import numpy as np, ml_dtypes
CORES = [2,3,42,43,82,83,122,123]
N = 8
BF = ml_dtypes.bfloat16
W, T, FC, SC, HB, RO, NB, LN = 4096, 128, 512, 256, 2048, 3, 4, 64
def pick(tab, ix):
    return np.take_along_axis(tab, ix[:, :, None, :], 3)
def hashes(hw, z):
    return np.sum(hw * z, axis=-2) & (HB - 1)
def compose(a, b):
    return (((a * b) >> 5) + a + 37 * b) & (W - 1)
def parts(rng):
    x = rng.integers(0, 256, (N, 8, 16, W)); x[:, :, 15] = rng.integers(0, 16, (N, 8, W))
    fw = rng.integers(0, W, (N, 8, 16, FC)); sw = rng.integers(0, W, (N, 8, 16, SC)); aw = rng.integers(0, W, (N, 8, 16, SC))
    z = rng.integers(0, 256, (N, 8, 16, T)); z[:, :, 15] = 0
    q = rng.integers(0, W, (N, 8, T)); hw = rng.integers(1, 256, (N, 8, 16, 1)); hw[:, :, 15] = 0
    th = rng.integers(800, 1101, (N, 8, 1))
    return x, fw, sw, aw, z, q, hw, th
def pack(x, fw, sw, aw, z, q, hw, th):
    return {"lx": x.reshape(N, 128, W).astype(np.float32).astype(BF), "fw": fw.reshape(N, 128, FC).astype(np.int32), "sw": sw.reshape(N, 128, SC).astype(np.int32), "aw": aw.reshape(N, 128, SC).astype(np.int32),
            "z0": z.reshape(N, 128, T).astype(np.float32).astype(BF), "q0": q.astype(np.int32), "hw": hw.reshape(N, 128, 1).astype(np.int32), "th": th.astype(np.int32)}
def setup_inputs(rng):
    return pack(*parts(rng))
def setup_inputs_spread(rng):
    x, fw, sw, aw, z, q, hw, th = parts(rng)
    x[:, :, :15] = (np.exp2(8 * rng.random((N, 8, 1, W))) * rng.random((N, 8, 15, W))).astype(np.int64); x[:, :, 15] = (16 * rng.random((N, 8, W)) ** 2).astype(np.int64)
    z[:, :, :15] = (np.exp2(8 * rng.random((N, 8, 1, T))) * rng.random((N, 8, 15, T))).astype(np.int64)
    e = rng.choice(np.array([1.0, 2.0, 4.0]), (N, 8, 1, 1))
    fw, sw, aw = [np.minimum((W * rng.random(v.shape) ** e).astype(np.int64), W - 1) for v in (fw, sw, aw)]
    q = np.minimum((W * rng.random(q.shape) ** e[..., 0]).astype(np.int64), W - 1)
    hw[:, :, :15] = (np.exp2(8 * rng.random((N, 8, 15, 1))) * rng.random((N, 8, 15, 1))).astype(np.int64)
    th = rng.choice(np.array([150, 250, 400, 800, 1300, 2500, 4095]), (N, 8, 1))
    return pack(x, fw, sw, aw, z, q, hw, th)
def setup_inputs_ends(rng):
    def two(hi, *shape):
        return hi * rng.integers(0, 2, shape)
    x = two(255, N, 8, 16, W); k = rng.integers(0, 3, (N, 8, 1, W)); x = np.where(k == 0, x, np.where(k == 1, 0, 255)); x[:, :, 15] = two(15, N, 8, W)
    fw = two(W - 1, N, 8, 16, FC); sw = two(W - 1, N, 8, 16, SC); aw = two(W - 1, N, 8, 16, SC); sw[..., SC - 1] = W - 1; aw[..., SC - 1] = W - 1
    z = two(255, N, 8, 16, T); k = rng.integers(0, 3, (N, 8, 1, T)); z = np.where(k == 0, z, np.where(k == 1, 0, 255)); z[..., T - 1] = 255
    q = two(W - 1, N, 8, T); hw = two(255, N, 8, 16, 1); hw[:, 7] = 255; hw[:, 0, 0] = 0
    hw[:, 6] = 0; hw[:, 6, 0] = 255; hw[:, 6, 1] = 2; hw[:, :, 15] = 0
    th = np.full((N, 8, 1), 4095); used = np.array([0, W - 1, W - 37, compose(W - 1, W - 1)])
    for a in range(N):
        for g in range(8):
            m = (g + N - 1 - a) % 4
            if m == 0:
                x[a, g][:, 0] = 0; x[a, g][:15, W - 1] = 255; x[a, g, 15, W - 1] = 15
                if g < 4: th[a, g] = 0
            elif m == 2:
                x[a, g][:15, used] = 255; x[a, g][15, used] = 15
            elif m == 3:
                x[a, g][:, used] = 0; z[a, g][:, T // 2:] = 255
    z[:, :, 15] = 0
    return pack(x, fw, sw, aw, z, q, hw, th)
def setup_inputs_corners(rng):
    x, fw, sw, aw, z, q, hw, th = parts(rng); x[:, :, 15] = rng.choice(np.array([0, 1, 13, 14, 15]), (N, 8, W))
    for a in range(N):
        for g in range(8):
            m = (a + g) % 4
            if m == 0:
                v = rng.permutation(W)[:T]; d = rng.integers(99, 102, T); y = np.array(z[a, g]); y[0] = np.where(y[0] < 128, y[0] + d, y[0] - d); y[15] = 15
                x[a, g][:, v] = y; q[a, g] = v; th[a, g] = 100
            elif m == 1:
                h = hashes(hw[a, g], z[a, g]); fw[a, g][:, h >> 2] = compose(sw[a, g][:, h & (SC - 1)], aw[a, g][:, h >> 3]); th[a, g] = 4095
            elif m == 2:
                fw[a, g] = rng.choice(np.array([0, 1, W - 2, W - 1]), (16, FC)); q[a, g] = np.arange(T); hw[a, g, :15] = 255 * (a & 1); th[a, g] = 1200
            else:
                x[a, g][:15] = 128; th[a, g] = 1000
    return pack(x, fw, sw, aw, z, q, hw, th)
def setup_inputs_crowd(rng):
    x, fw, sw, aw, z, q, hw, th = parts(rng); mid = rng.integers(0, 80, (N, 8, 15, 1))
    for a in range(N):
        for g in range(8):
            t = int(rng.integers(0, T)); odd = np.array(z[a, g][:, t]); one = np.array(z[a, g][:, (t + 1) % T]); full = np.array(one); full[15] = 15
            if g == 4 or g == 5:
                to = (a + 1 + np.arange(T) // (T // NB)) % N; e = rng.multinomial(T - rng.integers(0, 3, T), np.full(15, 1.0 / 15)).T
                x[a, g][:15] = mid[a, g]; z[a, g][:15] = np.minimum(mid[a, g] + mid[:, g, :, 0][to].T + e, 255); th[a, g] = g - 4
                if g == 5: z[a, g][:15, t] = mid[a, g, :, 0]; x[a, g, 15, q[a, g, t]] = 15
            elif g == 7 and a & 1:
                hw[a, g] = 0; hw[a, g, 0] = 8; hw[a, g, 1] = 1; th[a, g] = 4095
                y = rng.integers(96, 160, (16, T)); y[0] = rng.permutation(256)[:T]; y[1] = rng.integers(0, 8, T); y[15] = 0; z[a, g] = y
                h = hashes(hw[a, g], y)[:LN]; cs = compose(sw[a, g][:, h & (SC - 1)], aw[a, g][:, h >> 3]); near = np.isin(np.arange(W), cs); rest = np.flatnonzero(~near)
                x[a, g][2:15] = np.where(near, rng.integers(96, 160, (13, W)), 255 * rng.integers(0, 2, (13, W))); x[a, g][15] = np.where(near, 15, 0)
                fw[a, g][:, h >> 2] = rng.choice(rest, (16, LN)); q[a, g, :LN] = rng.choice(rest, LN)
            elif g == 7:
                z[a, g] = z[a, g][:, np.arange(T) & 3]; th[a, g] = 4095
            else:
                z[a, g] = one[:, None]; h = int(hashes(hw[a, g], one[:, None])[0]); cs = compose(sw[a, g][:, h & (SC - 1)], aw[a, g][:, h >> 3])
                if g < 2:
                    v = int(rng.integers(0, W)); x[a, g][:, v] = full; q[a, g] = v; th[a, g] = 1
                elif g < 4:
                    v = int(cs[5]); o = (v + 1) & (W - 1); x[a, g][:, v] = full; q[a, g] = o; c = fw[a, g][:, h >> 2]; fw[a, g][:, h >> 2] = np.where(c == v, o, c); th[a, g] = 4095 if g == 2 else 1
                else:
                    p = rng.permutation(W); p = p[~np.isin(p, cs)][:T]; x[a, g][:, p] = full[:, None]; q[a, g] = p; fw[a, g][:, h >> 2] = cs; th[a, g] = 4095
                if g in (1, 3): z[a, g][:, t] = odd
    return pack(x, fw, sw, aw, z, q, hw, th)
def setup_inputs_ties(rng):
    x, fw, sw, aw, z, q, hw, th = parts(rng)
    x[:, :, :15] = rng.integers(100, 102, (N, 8, 15, W)); x[:, :, 15] = rng.integers(3, 5, (N, 8, W)); z[:, :, :15] = rng.integers(100, 102, (N, 8, 15, T)); th = rng.integers(178, 187, (N, 8, 1))
    x[:, 2::3, :15] = rng.integers(0, 4, (N, 2, 15, W)); x[:, 2::3, 15] = 0; th[:, 2::3] = rng.integers(3985, 4006, (N, 2, 1))
    less = (np.arange(T) & 7) == rng.integers(0, 8, (N, 2, 1, 1))
    z[:, 2::3, :15] = np.where(less, rng.integers(200, 256, (N, 2, 15, T)), rng.integers(254, 256, (N, 2, 15, T)))
    mid = rng.integers(140, 160, (N, 8, 15)); goal = 2049 + 2 * rng.integers(0, 4, (N, 8))
    for a in range(N):
        to = (a + 1 + np.arange(T) // (T // NB)) % N
        for g in (1, 6):
            n = (a + g // 3) % 4
            least = goal[to, g] + rng.integers(-2, 2, T)
            d = rng.multinomial(np.sum(mid[to, g], axis=1) - least, np.full(15, 1.0 / 15)).T
            x[a, g][:15] = mid[a, g][:, None]; x[a, g][15] = 15; z[a, g][:15] = np.minimum(mid[a, g][:, None] + d, 255)
            z[a, g][:, rng.permutation(T)[:n]] = 0; th[a, g] = goal[a, g] - n
    return pack(x, fw, sw, aw, z, q, hw, th)
def check_inputs(d):
    bad = []
    for k, lo, hi in (("lx", 0, 255), ("fw", 0, W - 1), ("sw", 0, W - 1), ("aw", 0, W - 1), ("z0", 0, 255), ("q0", 0, W - 1), ("hw", 0, 255), ("th", 0, 4095)):
        v = np.asarray(d[k]).astype(np.float64)
        if not (np.min(v) >= lo and np.max(v) <= hi): bad.append("range of " + k)
        elif np.any(v != np.floor(v)): bad.append("whole numbers of " + k)
    for k, hi in (("lx", 15), ("z0", 0), ("hw", 0)):
        v = np.asarray(d[k]).astype(np.float64)[:, 15::16]
        if not np.max(v) <= hi: bad.append("rows 16*g + 15 of " + k)
    return bad
def reference(lx, fw, sw, aw, z0, q0, hw, th):
    x = lx.astype(np.float32).astype(np.int64).reshape(N, 8, 16, W); fd = fw.astype(np.int64).reshape(N, 8, 16, FC)
    sd = sw.astype(np.int64).reshape(N, 8, 16, SC); ad = aw.astype(np.int64).reshape(N, 8, 16, SC)
    z = z0.astype(np.float32).astype(np.int64).reshape(N, 8, 16, T); q = q0.astype(np.int64).reshape(N, 8, T)
    wt = hw.astype(np.int64).reshape(N, 8, 16, 1); lim = th.astype(np.int64).reshape(N, 8, 1); none = np.zeros((N, 8, 1), np.int64)
    own = (np.arange(T)[None, :] & 15) == np.arange(16)[:, None]; BL = T // NB
    for s in range(RO):
        h = hashes(wt, z); col = h >> 2
        stored = np.where(own, q[:, :, None, :], pick(fd, col)); comp = compose(pick(sd, h & (SC - 1)), pick(ad, h >> 3))
        names = np.concatenate([stored, comp], axis=2)
        words = pick(x, names.reshape(N, 8, 32 * T)).reshape(N, 8, 16, 32, T)
        tm = np.sum(np.abs(words[:, :, :15] - z[:, :, :15, None, :]), axis=2) + 16 * (15 - words[:, :, 15])
        bs = np.argmin(tm[:, :, :16], axis=2); bc = 16 + np.argmin(tm[:, :, 16:], axis=2); slow = np.argmax(tm[:, :, :16], axis=2)
        ts, tc = [np.take_along_axis(tm, b[:, :, None, :], 2)[:, :, 0] for b in (bs, bc)]
        cw = tc < ts; win = np.minimum(ts, tc) < lim + none
        wn = np.take_along_axis(names, np.where(cw, bc, bs)[:, :, None, :], 2)[:, :, 0]; ln = np.take_along_axis(names, np.where(cw, bs, bc)[:, :, None, :], 2)[:, :, 0]
        xw = pick(x, wn); top = np.max(words[:, :, :, 16:], axis=3)
        xn = np.array(x); fn = np.array(fd); lo = LN * (s % (T // LN))
        for a in range(N):
            for g in range(8):
                le = np.arange(lo, lo + LN); le = le[win[a, g, le]]
                v = ln[a, g, le]; xn[a, g, 15, v] = np.maximum(x[a, g, 15, v] - 1, 0)
                v, i = np.unique(wn[a, g, le], return_index=True); t = le[i]
                xn[a, g][:15, v] = (x[a, g][:15, v] + z[a, g][:15, t]) >> 1; xn[a, g][15, v] = np.minimum(x[a, g][15, v] + 2, 15)
                le = le[cw[a, g, le]]; c, i = np.unique(col[a, g, le], return_index=True); t = le[i]
                fn[a, g][slow[a, g, t], c] = wn[a, g, t]
        z = np.abs(z - np.where(win[:, :, None, :], xw, top)); z[:, :, 15] = 0
        q = np.where(win, wn, q); none = T - np.sum(win.astype(np.int64), axis=2, keepdims=True); x, fd = xn, fn
        if s < RO - 1:
            z2, q2 = np.zeros_like(z), np.zeros_like(q)
            for a in range(N):
                for b in range(NB):
                    to = (a + 1 + b + s) % N; z2[to, :, :, b * BL:(b + 1) * BL] = z[a, :, :, b * BL:(b + 1) * BL]; q2[to, :, b * BL:(b + 1) * BL] = q[a, :, b * BL:(b + 1) * BL]
            z, q = z2, q2
    return {"yx": x.reshape(N, 128, W).astype(np.float32).astype(BF), "yf": fd.reshape(N, 128, FC).astype(np.float32), "yz": z.reshape(N, 128, T).astype(np.float32).astype(BF), "yq": q.astype(np.float32)}

@@ -1,0 +1,726 @@
+from concourse.bass import DstId, RemoteDMATransfer
+from concourse.mybir import dt, AluOpType, ActivationFunctionType
+
+N, STEPS, NB = 8, 3, 4
+BIG = 33554432.0
+F32, BF, I32, U16 = "float32", "bfloat16", "int32", "uint16"
+OPT = {"light": False, "shift": [1, 0, 0], "classes": 4, "cut": 96, "hib": 0, "kfirst": 0, "cm_early": False, "defer": 0,
+       "hash0": "hkhkhhhkhl", "hash": "hkhhhhh", "order0": "fcfcfclclc", "order": "fcfcfckckc", "plan": "wewewwewew", "last_plan": "wewewwww"}
+
+
+def _s(cols, dtype, parts=128):
+    return ("sbuf", [parts, cols], dtype)
+
+
+SCRATCH = {
+    "X": _s(4160, BF), "FW": _s(576, F32), "fwi": _s(512, I32), "swi": _s(256, I32), "awi": _s(256, I32),
+    "Sp": _s(256, F32), "LP": _s(256, F32), "zin": _s(128, BF), "L1": _s(256, BF), "L2": _s(256, BF),
+    "pay0": _s(256, BF), "pay1": _s(256, BF), "zout": _s(128, BF), "qout": _s(128, F32),
+    "hwi": _s(8, I32), "thi": _s(8, I32), "thr": _s(16, F32), "c1088": _s(16, BF), "onef": _s(128, F32),
+    "qi": _s(128, I32), "qb": _s(256, I32), "qh": _s(256, BF),
+    "pi": _s(8, I32), "pm": _s(8, I32), "col": _s(16, F32), "G8": _s(16, BF),
+    "J16": _s(128, F32), "Jd": _s(16, F32), "vc": _s(256, F32),
+    "BM": _s(128, BF), "Hb": _s(128, BF), "SU": _s(128, F32), "SO": _s(192, F32), "rneg": _s(192, F32),
+    "Bk": _s(48, BF), "own": _s(256, BF), "nown": _s(128, F32), "nbig": _s(192, BF), "o16": _s(128, BF),
+    "idf": _s(128, F32), "idb": _s(128, BF), "id64": _s(128, BF), "NI": _s(256, BF), "E0": _s(128, BF), "E8": _s(128, BF), "Ex": _s(128, BF),
+    "E64": _s(128, BF), "I8": _s(16, BF), "I2": _s(256, BF), "rmin": _s(256, F32), "rmax": _s(128, F32), "rM": _s(2048, BF),
+    "ZO": _s(16, U16), "CK": _s(512, BF), "on": _s(128, BF), "s64": _s(128, BF), "c32": _s(128, BF), "cm": _s(768, BF), "DU": _s(24, F32),
+    "ui": _s(8, I32), "hb": _s(24, I32), "ho": _s(24, U16), "A1": _s(128, F32), "pr": _s(128, F32), "xi": _s(128, I32),
+    "ci": _s(128, I32), "t1": _s(128, F32), "nf": _s(256, F32), "hib": _s(256, BF), "off": _s(256, U16),
+    "zx": _s(2048, BF), "WF": _s(2048, BF), "RC": _s(2048, BF), "Dw": _s(6144, BF), "Fr": _s(64, F32),
+    "SF": _s(256, F32), "SC": _s(256, F32), "SX": _s(128, F32), "m1": _s(16, F32), "R": _s(32, I32),
+    "E": _s(256, BF), "zo": _s(8, U16), "ut": _s(8, I32), "jt": _s(8, I32), "P6": _s(80, I32), "Pb": _s(88, BF),
+    "te": _s(8, F32), "LE": _s(8, U16),
+    "IV": _s(24, BF), "IK": _s(16, BF), "CP": _s(448, BF), "RO": _s(192, F32), "nb": _s(16, F32), "EQ": _s(768, BF), "SD": _s(768, BF),
+    "to": _s(16, F32), "tm": _s(16, F32), "LO": _s(16, U16), "xl": _s(64, BF), "xs": _s(64, F32), "xh": _s(64, I32), "xw": _s(64, BF),
+    "d1": _s(64, F32), "oh": _s(64, F32), "d2": _s(64, F32),
+    "DD": ("psum", [128, 2048], F32),
+    "KF": ("psum", [128, 512], F32), "KC": ("psum", [128, 512], F32), "M1": ("psum", [128, 512], F32), "M2": ("psum", [128, 512], F32),
+}
+BANKS = ("D0", "D1", "D2", "D3", "KF", "KC", "M1", "M2")
+NDMA = 14
+SEMAPHORES = ["qv", "qa", "qp", "qg", "arr1", "arr2", "sent0", "sent1"] + ["d%d" % i for i in range(NDMA)]
+
+
+def travel_engines(T, topo, rank, s):
+    src = T.cores[rank]
+    dsts = [T.cores[(rank + 1 + b + s) % N] for b in range(NB)]
+    common = [e for e in topo.engines(src, dsts[0]) if all(e in topo.engines(src, d) for d in dsts)]
+    per = 1
+    while 2 * per * NB <= len(common):
+        per *= 2
+    out = []
+    for b in range(NB):
+        m = 0
+        for e in common[b * per:(b + 1) * per]:
+            m |= 1 << e
+        out.append((dsts[b], m, per))
+    return out
+
+
+def rank_program(g, core, T, topo):
+    rank = T.rank_of(core)
+    if rank is None:
+        return
+    A, AF = AluOpType, ActivationFunctionType
+    Q = {"v": g.vector, "a": g.scalar, "p": g.tensor, "g": g, "s": g.sync}
+    QS = {"v": "qv", "a": "qa", "p": "qp", "g": "qg"}
+    count = {}
+    known = {q: {} for q in Q}
+    lastw, readers = {}, {}
+    ndma = [0]
+
+    def wait(q, tok):
+        sem, val, clock = tok[0], tok[1], tok[2]
+        if known[q].get(sem, 0) >= val:
+            return
+        Q[q].wait_ge(T.sem[sem], val)
+        known[q][sem] = val
+        for k, v in clock.items():
+            if known[q].get(k, 0) < v:
+                known[q][k] = v
+
+    def order(q, r, w):
+        deps = []
+        for k in r:
+            if k in lastw:
+                deps.append(lastw[k])
+            if k in BANKS:
+                deps += [t for t in readers.get(k, []) if t[3] != q]
+        for k in w:
+            if k in lastw and not (k in BANKS and q == "p" and lastw[k][3] == "p"):
+                deps.append(lastw[k])
+            deps += readers.get(k, [])
+        deps.sort(key=lambda t: -t[1])
+        for t in deps:
+            wait(q, t)
+
+    def note(tok, r, w):
+        for k in r:
+            readers.setdefault(k, []).append(tok)
+        for k in w:
+            lastw[k] = tok
+            readers[k] = []
+
+    def op(q, call, r, w):
+        order(q, r, w)
+        sem = QS[q]
+        count[sem] = count.get(sem, 0) + 1
+        call().then_inc(T.sem[sem], 1)
+        note((sem, count[sem], dict(known[q]), q), r, w)
+
+    def dma(q, out, in_, r, w):
+        order(q, r, w)
+        sem = "d%d" % ndma[0]
+        ndma[0] += 1
+        count[sem] = 16
+        Q[q].dma_start(out, in_).then_inc(T.sem[sem], 16)
+        note((sem, 16, dict(known[q]), "dma"), r, w)
+
+    V_ = g.vector
+
+    def ts(out, in0, s1, s2, o0, o1, r, w):
+        if o1 is None:
+            op("v", lambda: V_.tensor_scalar(out, in0, s1, None, o0), r, w)
+        else:
+            op("v", lambda: V_.tensor_scalar(out, in0, s1, s2, o0, o1), r, w)
+
+    def tt(out, in0, in1, o, r, w):
+        op("v", lambda: V_.tensor_tensor(out, in0, in1, o), r, w)
+
+    def cp(out, in_, r, w):
+        op("v", lambda: V_.tensor_copy(out, in_), r, w)
+
+    def ms(ap, c, w):
+        op("v", lambda: V_.memset(ap, c), [], w)
+
+    def scan(out, d0, d1, o0, o1, r, w):
+        op("v", lambda: V_.tensor_tensor_scan(out, d0, d1, 0.0, o0, o1), r, w)
+
+    def act(out, in_, f, r, w, **kw):
+        op("a", lambda: g.scalar.activation(out, in_, f, **kw), r, w)
+
+    def lin(out, in_, scale, bias, r, w):
+        act(out, in_, AF.Identity, r, w, scale=scale, bias=bias)
+
+    def mm(out, lhsT, rhs, start, stop, r, w):
+        op("p", lambda: g.tensor.matmul(out, lhsT, rhs, start, stop), r, w)
+
+    def iota(out, pat, base, cm, w, flag=True):
+        if flag:
+            op("g", lambda: g.iota(out, pat, base, cm, allow_small_or_imprecise_dtypes=True), [], w)
+        else:
+            op("g", lambda: g.iota(out, pat, base, cm), [], w)
+
+    def sel(out, in_, pat, cmp, base, cm, r, w):
+        op("g", lambda: g.affine_select(out, in_, pat, cmp, 0.0, base, cm), r, w)
+
+    def zero(out, n, w):
+        iota(out, [[0, n]], 0, 0, w)
+
+    C = T.col
+    PM, HW, WT, ZB, ZS, C1, C2, CMX, CD, JC, P16, IS15, CB, C3 = [C[:, i:i + 1] for i in range(14)]
+    DD = T.DD
+
+    dma("s", T.zin[:], T.z0[:], [], ["zin"])
+    dma("a", T.hwi[:, 0:1], T.hw[:], [], ["hwi"])
+    dma("s", T.awi[:], T.aw[:], [], ["awi"])
+    dma("a", T.qi[0:8, :], T.q0[:], [], ["qi"])
+    dma("s", T.swi[:], T.sw[:], [], ["swi"])
+    dma("a", T.fwi[:], T.fw[:], [], ["fwi"])
+    dma("s", T.X[:, 0:4096], T.lx[:], [], ["X"])
+    dma("a", T.thi[0:1, 0:8], T.th[:], [], ["thi"])
+
+    ms(T.on[:], 1.0, ["on"])
+    ms(T.c32[:], 32.0, ["c32"])
+    ms(T.s64[0:16, :], 64.0, ["s64"])
+    iota(T.pi[:, 0:1], [[0, 1]], 0, 1, ["pi"], False)
+    iota(T.J16[:], [[0, 8], [1, 16]], 0, 0, ["J16"])
+    sel(T.BM[:], T.on[:], [[-16, 8], [0, 16]], A.is_ge, 0, 1, ["on"], ["BM"])
+    sel(T.BM[:], T.BM[:], [[16, 8], [0, 16]], A.is_ge, 15, -1, ["BM"], ["BM"])
+    sel(T.idb[:], T.on[:], [[-1, 128]], A.is_equal, 0, 1, ["on"], ["idb"])
+    sel(T.E0[0:16, :], T.on[0:16, :], [[-1, 8], [0, 16]], A.is_equal, 0, 1, ["on"], ["E0"])
+    sel(T.E64[0:8, :], T.s64[0:8, :], [[-1, 8], [0, 16]], A.is_equal, 0, 1, ["s64"], ["E64"])
+    sel(T.I8[0:8, :], T.on[0:8, 0:16], [[-1, 16]], A.is_equal, 8, 1, ["on"], ["I8"])
+    iota(P16, [[0, 1]], 0, 16, ["P16"])
+    iota(T.CK[0:1, 256:512], [[-12480, 2], [0, 8], [64, 16]], 12288 + 1024, 0, ["CK1"])
+    iota(T.CK[0:1, 0:256], [[-12480, 2], [0, 8], [64, 16]], 12288, 0, ["CK0"])
+    iota(T.vc[:], [[16, 4], [1, 64]], -63, 0, ["vc"])
+    iota(T.Jd[:, 0:8], [[0, 2], [16, 4]], 4096 - 8192, 0, ["Jda"])
+    iota(T.Jd[:, 8:12], [[16, 4]], 512 - 8192, 0, ["Jdb"])
+    iota(T.rM[:], [[0, 128], [2048, 16]], -1024, 0, ["rM"])
+    zero(T.pay0[:], 256, ["pay0z", "pay0q"])
+    sel(T.E8[0:16, :], T.s64[0:16, :], [[-1, 8], [0, 16]], A.is_equal, -8, 1, ["s64"], ["E8"])
+    sel(T.I2[:, 0:64], T.on[:, 0:64], [[1, 64]], A.is_equal, -63, 1, ["on"], ["I20a"])
+    sel(T.I2[:, 64:128], T.on[:, 0:64], [[-1, 64]], A.is_equal, 0, 1, ["on"], ["I20b"])
+    zero(T.IV[:, 0:8], 8, ["IVz"])
+    zero(T.IK[:, 0:8], 8, ["IKz"])
+    zero(T.Pb[:, 80:88], 8, ["Pbz"])
+    zero(T.X[:, 4096:4160], 64, ["Xd"])
+    zero(T.FW[:, 512:576], 64, ["FWd"])
+
+    ts(T.pm[:, 0:1], T.pi[:, 0:1], 15, None, A.bitwise_and, None, ["pi"], ["pm"])
+    ms(T.onef[0:1, :], 1.0, ["onef"])
+    cp(PM, T.pm[:, 0:1], ["pm"], ["PM"])
+    ms(T.c1088[0:1, :], -1088.0, ["c1088"])
+    ts(IS15, PM, 15.0, None, A.is_equal, None, ["PM"], ["IS15"])
+    ts(T.nown[:], T.J16[:], PM, None, A.not_equal, None, ["J16", "PM"], ["nown"])
+    ts(T.own[:, 0:128], T.J16[:], PM, None, A.is_equal, None, ["J16", "PM"], ["own0"])
+    ts(T.rneg[:, 0:128], T.J16[:], 0.0, -BIG, A.is_equal, A.mult, ["J16"], ["rneg"])
+    ts(T.ZO[:], T.J16[:, 0:16], 1.0, None, A.mult, None, ["J16"], ["ZO0"])
+    cp(HW, T.hwi[:, 0:1], ["hwi"], ["HW"])
+    ts(T.Hb[:], T.BM[:], HW, None, A.mult, None, ["BM", "HW"], ["Hb"])
+    ts(T.qb[0:8, 0:128], T.qi[0:8, :], 63, None, A.bitwise_and, None, ["qi"], ["qb0"])
+    ts(T.qb[0:8, 128:256], T.qi[0:8, :], 6, None, A.logical_shift_right, None, ["qi"], ["qb1"])
+    lin(ZB, IS15, 15.0, 0.0, ["IS15"], ["ZB"])
+    lin(WT, IS15, 61440.0, 4096.0, ["IS15"], ["WT"])
+    lin(ZS, IS15, -1.0, 1.0, ["IS15"], ["ZS"])
+    lin(T.nbig[:, 0:128], T.nown[:], -1048576.0, 0.0, ["nown"], ["nbig"])
+    lin(T.NI[:, 0:128], T.idb[:], -1.0, 0.0, ["idb"], ["NI0"])
+
+    def race_consts():
+        lin(T.NI[:, 128:256], T.idb[:], 1.0 / 64, 0.0, ["idb"], ["NI1"])
+        lin(T.idf[:], T.idb[:], 1.0, 0.0, ["idb"], ["idf"])
+        lin(T.Bk[:, 0:8], T.BM[:, 0:128:16], WT, 0.0, ["BM", "WT"], ["Bk"])
+        lin(T.Bk[:, 8:16], T.BM[:, 0:128:16], WT, 0.0, ["BM", "WT", "Bk"], ["Bk"])
+        act(T.rmin[:, 0:128], T.J16[:], AF.Relu, ["J16"], ["rmin0"], scale=-BIG, bias=BIG)
+        lin(T.Bk[:, 16:32], T.Bk[:, 0:16], 2.0, 0.0, ["Bk"], ["Bk2"])
+        lin(T.Bk[:, 32:48], T.Bk[:, 0:16], -1.0, 0.0, ["Bk"], ["Bkn"])
+        act(T.rmin[:, 128:256], T.J16[:], AF.Relu, ["J16"], ["rmin1"], scale=-BIG, bias=BIG)
+        lin(T.own[:, 128:256], T.own[:, 0:128], 1.0, 0.0, ["own0"], ["own1"])
+        lin(T.G8[:, 0:8], T.BM[:, 0:128:16], 1.0, 0.0, ["BM"], ["G8a"])
+        lin(T.G8[:, 8:16], T.BM[:, 0:128:16], 2.0, 0.0, ["BM"], ["G8b"])
+        lin(T.o16[:], T.own[:, 0:128], P16, 0.0, ["own0", "P16"], ["o16"])
+
+    def learn_consts_a():
+        lin(T.rmax[:], T.rmin[:, 0:128], -1.0, 128.0, ["rmin0"], ["rmax"])
+        lin(CB, PM, -8192.0, 8192.0, ["PM"], ["CB"])
+        lin(T.nbig[:, 128:192], T.nown[:, 0:64], -1048576.0, 0.0, ["nown", "nbig"], ["nbig"])
+        lin(T.rneg[:, 128:192], T.rmin[:, 0:64], -1.0, 0.0, ["rmin0", "rneg"], ["rneg"])
+        lin(T.DU[:, 0:12], T.Jd[:, 0:12], 1.0, PM, ["Jda", "Jdb", "PM"], ["DU"])
+        lin(JC, PM, -1.0, 30.0, ["PM"], ["JC"])
+        lin(T.DU[:, 16:24], T.DU[:, 0:8], 1.0, 8192.0, ["DU"], ["DUe"])
+        lin(CD, IS15, -1.0, 0.0, ["IS15"], ["CD"])
+        lin(C1, IS15, 0.5, 0.5, ["IS15"], ["C1"])
+        lin(C2, IS15, 2.25, -0.25, ["IS15"], ["C2"])
+        lin(C3, IS15, -12.75, -0.25, ["IS15"], ["C3"])
+        lin(CMX, IS15, -240.0, 255.0, ["IS15"], ["CMX"])
+
+    def learn_consts_b():
+        for k in range(3):
+            act(T.cm[:, 256 * k:256 * k + 256], T.vc[:], AF.Relu, ["vc", "CB"], ["cm%d" % k], scale=-8192.0, bias=CB)
+
+    def later_consts():
+        sel(T.I2[:, 128:192], T.on[:, 0:64], [[1, 64]], A.is_equal, -127, 1, ["on"], ["I21a"])
+        sel(T.I2[:, 192:256], T.on[:, 0:64], [[-1, 64]], A.is_equal, -64, 1, ["on"], ["I21b"])
+        zero(T.pay1[:], 256, ["pay1z", "pay1q"])
+
+    def step(s, late):
+        def fill(n=1):
+            for _ in range(n):
+                if late:
+                    late.pop(0)()
+
+        lam = s % 2
+        last = s == STEPS - 1
+        if s == 0:
+            zk, Z, zs, zob, zok = "zin", T.zin, 1, 0, "ZO0"
+        else:
+            zk, Z, zs, zob, zok = "L%d" % s, T["L%d" % s], 2, 128, "ZO1"
+            got = sum(m[2] for r2 in range(N) for m in travel_engines(T, topo, r2, s - 1) if m[0] == core)
+            count["arr%d" % s] = got
+            note(("arr%d" % s, got, {}, "remote"), [], [zk])
+
+        def zc(a, b, step=1):
+            return Z[:, zs * a:zs * b:zs * step]
+
+        mm(T.M1[:, 0:128], T.idb[:], T.nbig[:, 0:128], True, False, ["idb", "nbig"], ["M1"])
+        mm(T.M1[:, 0:128], T.Hb[:], zc(0, 128), False, True, [zk, "Hb"], ["M1"])
+        mm(T.M2[:, 128:136], zc(0, 128), T.Hb[:, 0:128:16], True, True, [zk, "Hb"], ["M2"])
+        zall = ["zx%d" % c for c in range(4)]
+
+        def repeat(q, t0, t1):
+            keys = ["zq%s%d" % (q, j) for j in range(5)]
+            for j, (o, st) in enumerate(((0, 16), (8, 16), (4, 8), (2, 4), (1, 2))):
+                dst = T.zx[:, 16 * t0 + o:16 * t1:st]
+                src = zc(t0, t1) if j < 2 else T.zx[:, 16 * t0:16 * t1:st]
+                rd = [zk] if j < 2 else keys[:j]
+                wr = [keys[j]] + (zall if j == 0 else [])
+                if q == "g":
+                    n = (t1 - t0) * 16 // st
+                    op("g", lambda: g.affine_select(dst, src, [[0, n]], A.is_ge, 0.0, 0, 0), rd, [keys[j]])
+                elif s == 0 and j < 2:
+                    act(dst, src, AF.Identity, rd + ["ZB"], wr, bias=ZB)
+                else:
+                    act(dst, src, AF.Identity, rd, wr)
+            return keys
+
+        cut = 128 if s == 0 else OPT["cut"]
+        if cut < 128:
+            order("g", [], zall)
+        zx_keys = repeat("a", 0, cut) + (repeat("g", cut, 128) if cut < 128 else []) + zall
+        if s == 0:
+            cp(T.qh[0:8, :], T.qb[0:8, :], ["qb0", "qb1"], ["qh"])
+            ts(T.LP[:], T.awi[:], 3232.0, -6619136.0, A.mult, A.add, ["awi"], ["LP"])
+        chain_h = [
+            lambda: scan(T.SU[:], T.rneg[:, 0:128], T.M1[:, 0:128], A.add, A.max, ["rneg", "M1"], ["SU"]),
+            lambda: cp(T.ui[:], T.SU[:, 15:128:16], ["SU"], ["ui"]),
+            lambda: ts(T.hb[:, 16:24], T.ui[:], 2, 511, A.logical_shift_right, A.bitwise_and, ["ui"], ["hb2"]),
+            lambda: ts(T.hb[:, 0:8], T.ui[:], 3, 255, A.logical_shift_right, A.bitwise_and, ["ui"], ["hb0"]),
+            lambda: ts(T.hb[:, 8:16], T.ui[:], 255, None, A.bitwise_and, None, ["ui"], ["hb1"]),
+            lambda: cp(T.ho[:], T.hb[:], ["hb0", "hb1", "hb2"], ["ho"])]
+        chain_k = [
+            lambda: cp(T.ut[:], T.M2[:, 128:136], ["M2"], ["ut"]),
+            lambda: ts(T.P6[:, 56:64], T.ut[:], 2, 63, A.logical_shift_right, A.bitwise_and, ["ut"], ["P6k"]),
+            lambda: ts(T.P6[:, 64:72], T.ut[:], 8, 7, A.logical_shift_right, A.bitwise_and, ["ut"], ["P6h"])]
+        if s == 0:
+            late = [lambda: ts(T.Sp[:], T.swi[:], -2048.0, None, A.add, None, ["swi"], ["Sp"])]
+        for ch in (OPT["hash0"] if s == 0 else OPT["hash"]):
+            if ch == "h":
+                chain_h.pop(0)()
+            elif ch == "k":
+                chain_k.pop(0)()
+            else:
+                fill()
+        mm(T.M2[:, 0:128], T.idb[:], T.nbig[:, 0:128], True, False, ["idb", "nbig"], ["M2"])
+        if s == 0:
+            mm(T.M2[:, 0:128], T.E0[0:8, :], T.qh[0:8, 0:128], False, False, ["E0", "qh"], ["M2"])
+            mm(T.M2[:, 0:128], T.E64[0:8, :], T.qh[0:8, 128:256], False, True, ["E64", "qh"], ["M2"])
+        else:
+            mm(T.M2[:, 0:128], T.Ex[0:16, :], Z[0:16, 1:256:2], False, True, ["Ex", zk], ["M2"])
+        nF = 4 - OPT["shift"][s]
+        for c in range(nF):
+            mm(DD[:, 512 * c:512 * c + 512], T.NI[:, 0:128], T.zx[:, 512 * c:512 * c + 512], True, False, ["NI0"] + zx_keys, ["D%d" % c])
+        Fw, fk = (T.fwi[:], "fwi") if s == 0 else (T.FW[:, 0:512], "FW")
+        chain_f = [
+            lambda: tt(T.t1[:], Fw.indirect(T.ho[:, 16:24]), T.nown[:], A.mult, [fk, "ho", "nown"], ["t1"]),
+            lambda: tt(T.nf[:, 0:128], T.t1[:], T.M2[:, 0:128], A.max, ["t1", "M2"], ["nf0"]),
+            lambda: cp(T.off[:, 0:128], T.nf[:, 0:128], ["nf0"], ["off0"])]
+        chain_c = [
+            lambda: ts(T.A1[:], T.awi[:].indirect(T.ho[:, 0:8]), 32.0, None, A.add, None, ["awi", "ho"], ["A1"]),
+            lambda: tt(T.pr[:], T.Sp[:].indirect(T.ho[:, 8:16]), T.A1[:], A.mult, ["Sp", "ho", "A1"], ["pr"]),
+            lambda: tt(T.xi[:], T.LP[:].indirect(T.ho[:, 0:8]), T.pr[:], A.add, ["LP", "ho", "pr"], ["xi"]),
+            lambda: ts(T.ci[:], T.xi[:], 5, 4095, A.arith_shift_right, A.bitwise_and, ["xi"], ["ci"]),
+            lambda: cp(T.off[:, 128:256], T.ci[:], ["ci"], ["off1"])]
+        if s == 0:
+            late = [lambda: ts(T.thr[0:1, 0:8], T.thi[0:1, 0:8], 4096.0, None, A.mult, None, ["thi"], ["THa"]),
+                    lambda: ts(T.thr[0:1, 8:16], T.thi[0:1, 0:8], 4096.0, None, A.mult, None, ["thi"], ["THb"])]
+        for ch in (OPT["order0"] if s == 0 else OPT["order"]):
+            if ch == "f":
+                chain_f.pop(0)()
+            elif ch == "c":
+                chain_c.pop(0)()
+            elif ch == "k":
+                chain_k.pop(0)()
+            else:
+                fill()
+        fill(len(late))
+        cp(T.nf[:, 128:256], T.ci[:], ["ci"], ["nf1"])
+        if s == 0:
+            race_consts()
+            learn_consts_a()
+            if OPT["cm_early"]:
+                learn_consts_b()
+            cp(T.FW[:, 0:512], T.fwi[:], ["fwi"], ["FW"])
+
+        def old_column():
+            act(T.Fr[:], T.FW[:, 0:512].indirect(T.ho[:, 16 + 4 * lam:20 + 4 * lam]), AF.Identity, ["FW", "ho"], ["Fr"])
+
+        def upper(r):
+            act(T.hib[:, 128 * r:128 * r + 128], T.nf[:, 128 * r:128 * r + 128], AF.Identity, ["nf%d" % r], ["hib%d" % r], bias=12256.5)
+
+        if s > 0:
+            old_column()
+        upper(0)
+        VK = T.M1[:, 128:144]
+        mm(VK, T.on[0:1, :], T.c1088[0:1, :], True, False, ["on", "c1088"], ["M1"])
+        mm(VK, T.onef[0:1, :], T.thr[0:1, :], False, False, ["onef", "THa", "THb"], ["M1"])
+        if s == 0:
+            mm(VK, T.qh[0:8, 0:128], T.idb[0:8, 0:16], False, False, ["idb", "qh"], ["M1"])
+            mm(VK, T.qh[0:8, 128:256], T.I8[0:8, :], False, True, ["I8", "qh"], ["M1"])
+        else:
+            mm(VK, T.c32[:], T.IV[:, 8:24], False, False, ["c32", "IV"], ["M1"])
+            mm(VK, Z[0:16, 1:256:2], T.idb[0:16, 0:16], False, True, ["idb", zk], ["M1"])
+
+        Xw = T.X[:, 0:4096]
+        for r, K, k in ((1, T.KC, "KC"), (0, T.KF, "KF")):
+            mm(K[:, 0:256], T.on[0:1, :], T.CK[0:1, 256 * r:256 * r + 256], True, False, ["on", "CK%d" % r], [k])
+
+        def names(r, K, k):
+            mm(K[:, 0:256], T.hib[:, 128 * r:128 * r + 128], T.NI[:], False, False, ["hib%d" % r, "NI0", "NI1"], [k])
+            mm(K[:, 0:128], T.nf[:, 128 * r:128 * r + 128], T.idf[:], False, False, ["nf%d" % r, "idf"], [k])
+
+        for c in range(nF):
+            act(T.WF[:, 512 * c:512 * c + 512], Xw.indirect(T.off[:, 32 * c:32 * c + 32]), AF.Identity, ["X", "off0"], ["WF%d" % c])
+            mm(DD[:, 512 * c:512 * c + 512], T.idb[:], T.WF[:, 512 * c:512 * c + 512], False, True, ["idb", "WF%d" % c], ["D%d" % c])
+            if c == 0:
+                names(0, T.KF, "KF")
+            if c == min(1, nF - 1):
+                upper(1)
+            if c == min(2, nF - 1):
+                names(1, T.KC, "KC")
+        light = OPT["light"]
+        if light:
+            for h in range(2):
+                tt(T.Dw[:, 2048 + 1024 * h:3072 + 1024 * h], Xw.indirect(T.off[:, 128 + 64 * h:192 + 64 * h]), T.zx[:, 1024 * h:1024 * h + 1024],
+                   A.subtract, ["X", "off1"] + zx_keys, ["Dw1%d" % h] + (["Dw1"] if h else []))
+            for c in range(nF, 4):
+                tt(T.WF[:, 512 * c:512 * c + 512], Xw.indirect(T.off[:, 32 * c:32 * c + 32]), T.zx[:, 512 * c:512 * c + 512], A.subtract,
+                   ["X", "off0"] + zx_keys, ["WF%d" % c])
+            if s == 0:
+                old_column()
+            act(T.Dw[:, 0:512 * nF], DD[:, 0:512 * nF], AF.Abs, ["D%d" % j for j in range(nF)], ["Dw0s"])
+            for h in range(2):
+                act(T.RC[:, 1024 * h:1024 * h + 1024], T.Dw[:, 2048 + 1024 * h:3072 + 1024 * h], AF.Abs, ["Dw1%d" % h], ["RC%d" % h])
+            for c in range(nF, 4):
+                act(T.Dw[:, 512 * c:512 * c + 512], T.WF[:, 512 * c:512 * c + 512], AF.Abs, ["WF%d" % c], ["Dw0%d" % c])
+            dw0 = ["Dw0s", "Dw10", "Dw11"] + ["Dw0%d" % c for c in range(4)]
+            for i in range(16):
+                mm(T.KC[:, i:256:16], T.RC[:, i:2048:16], T.Bk[:, 0:16], False, i == 15, ["RC0", "RC1", "Bk"], ["KC"])
+            for i in range(16):
+                mm(T.KF[:, i:256:16], T.Dw[:, i:2048:16], T.Bk[:, 0:16], False, i == 15, dw0 + ["Bk"], ["KF"])
+        else:
+            if nF < 4:
+                tt(T.WF[:, 512 * nF:2048], Xw.indirect(T.off[:, 32 * nF:128]), T.zx[:, 512 * nF:2048], A.subtract,
+                   ["X", "off0"] + zx_keys, ["WF%d" % c for c in range(nF, 4)])
+                act(T.Dw[:, 512 * nF:2048], T.WF[:, 512 * nF:2048], AF.Abs, ["WF%d" % j for j in range(nF, 4)], ["Dw0s"])
+            tt(T.Dw[:, 2048:4096], Xw.indirect(T.off[:, 128:256]), T.zx[:], A.subtract,
+               ["X", "off1"] + zx_keys, ["Dw1"])
+            if s == 0:
+                old_column()
+            for i in range(16):
+                mm(T.KC[:, i:256:16], T.Dw[:, 2048 + i:4096:16], T.Bk[:, 32:48], False, False, ["Dw1", "Bkn"], ["KC"])
+            ts(T.RC[:], T.Dw[:, 2048:4096], 0.0, None, A.max, None, ["Dw1"], ["RC"])
+            nc = OPT["classes"]
+            for c in range(nc):
+                act(T.Dw[:, c:512 * nF:nc], DD[:, c:512 * nF:nc], AF.Abs, ["D%d" % j for j in range(nF)], ["Dw0%d" % c])
+            dw0 = ["Dw0%d" % c for c in range(nc)] + ["Dw0s"]
+            for c in range(nc):
+                if c == OPT["kfirst"]:
+                    for i in range(16):
+                        mm(T.KC[:, i:256:16], T.RC[:, i:2048:16], T.Bk[:, 16:32], False, i == 15, ["RC", "Bk2"], ["KC"])
+                for i in range(c, 16, nc):
+                    mm(T.KF[:, i:256:16], T.Dw[:, i:2048:16], T.Bk[:, 0:16], False, i == 15, ["Dw0%d" % c, "Bk", "Dw0s"], ["KF"])
+
+        def greatest():
+            scan(T.Dw[:, 4096:6144], T.rM[:], T.Dw[:, 2048:4096], A.min, A.max, ["rM", "Dw1", "Dw10", "Dw11"], ["Dw2"])
+
+        if not last:
+            greatest()
+        scan(T.SC[:], T.rmin[:], T.KC[:, 0:256], A.add, A.min, ["rmin0", "rmin1", "KC"], ["SC"])
+        tt(T.m1[:], T.SC[:, 15:256:16], VK, A.min, ["SC", "M1"], ["m1"])
+        scan(T.SF[:], T.rmin[:], T.KF[:, 0:256], A.add, A.min, ["rmin0", "rmin1", "KF"], ["SF"])
+        tt(T.R[:, 0:16], T.SF[:, 15:256:16], T.m1[:], A.min, ["SF", "m1"], ["Rw"])
+        if s == 0 and not OPT["cm_early"]:
+            learn_consts_b()
+        if last:
+            lin(T.id64[:], T.idb[:], 64.0, 0.0, ["idb"], ["id64"])
+
+        pay = None if last else T["pay%d" % s]
+        pk = "pay%d" % s
+
+        def loser():
+            tt(T.R[:, 16:32], T.SF[:, 15:256:16], T.SC[:, 15:256:16], A.max, ["SF", "SC"], ["Rl"])
+
+        def place():
+            ts(T.P6[:, 0:8], T.R[:, 0:8], 6, 15, A.logical_shift_right, A.bitwise_and, ["Rw"], ["V0"])
+
+        def route():
+            ts(T.P6[:, 8:24], T.R[:, 0:16], 3072, None, A.bitwise_and, None, ["Rw"], ["V1"])
+
+        def move_b():
+            mm(DD[:, 0:8], T.o16[:], T.G8[:, 0:8], True, False, ["o16", "G8a"], ["D0"])
+            tt(T.E[:], T.P6[:, 0:16].indirect(T.ZO[:, 0:16]), T.own[:], A.mult, ["V0", "V1", "ZO0", "own0", "own1"], ["E"])
+            mm(DD[:, 0:8], T.E[:, 0:128], T.G8[:, 0:8], False, False, ["E", "G8a"], ["D0"])
+            mm(DD[:, 0:8], T.E[:, 128:256], T.G8[:, 8:16], False, True, ["E", "G8b"], ["D0"])
+
+        def move_q():
+            if last:
+                mm(T.M2[0:8, 0:128], T.Pb[:, 24:32], T.idb[:], True, False, ["Pbw", "idb"], ["M2"])
+                mm(T.M2[0:8, 0:128], T.Pb[:, 32:40], T.id64[:], False, True, ["Pbw", "id64"], ["M2"])
+            else:
+                mm(T.M2[0:16, 0:128], T.Pb[:, 24:40], T.idb[:], True, True, ["Pbw", "idb"], ["M2"])
+
+        def move_p():
+            cp(pay[0:16, 1:256:2], T.M2[0:16, 0:128], ["M2"], [pk + "q"])
+
+        def move_o():
+            cp(T.zo[:], DD[:, 0:8], ["D0"], ["zo"])
+
+        def move_z():
+            rd = dw0 + ["Dw1", "Dw2", "zo", "ZS"]
+            if last:
+                act(T.zout[:], T.Dw[:].indirect(T.zo[:]), AF.Abs, rd, ["zout"], scale=ZS)
+                dma("a", T.yz[:], T.zout[:], ["zout"], [])
+            else:
+                act(pay[:, 0:256:2], T.Dw[:].indirect(T.zo[:]), AF.Abs, rd + ["ZB"], [pk + "z"], scale=ZS, bias=ZB)
+
+        i2 = ["I2%da" % lam, "I2%db" % lam]
+        I2 = [T.I2[:, 128 * lam:128 * lam + 64], T.I2[:, 128 * lam + 64:128 * lam + 128]]
+
+        def flag_w():
+            ts(T.IV[:, 8:24], T.P6[:, 8:24], 2048.0, 128.0, A.is_ge, A.mult, ["V1"], ["IV"])
+
+        def flag_k():
+            ts(T.IK[:, 8:16], T.P6[:, 8:16], 1024.0, 128.0, A.not_equal, A.mult, ["V1"], ["IK"])
+
+        def keys(name, a, b):
+            return [name + str(k) for k in range(a, b)]
+
+        def compact(h, a, b):
+            c0, bank = (1024, "D2") if h == 0 else (512, "D1")
+            for k in range(a, b):
+                o = DD[0:16, c0 + 64 * k:c0 + 64 * k + 64]
+                mm(o, T.Pb[:, 24 + 16 * k:40 + 16 * k], I2[h], True, False, [("Pbw", "Pbl", "Pbk")[k], i2[h]], [bank])
+                if k < 2:
+                    mm(o, T.IV[:, 0:16], I2[h], False, True, ["IV", "IVz", i2[h]], [bank])
+                else:
+                    mm(o, T.IK[:], I2[h], False, True, ["IK", "IKz", i2[h]], [bank])
+
+        def copy_asc(a, b):
+            act(T.CP[0:16, 256 + 64 * a:256 + 64 * b], DD[0:16, 512 + 64 * a:512 + 64 * b], AF.Identity, ["D1"], keys("CPa", a, b))
+
+        def copy_desc(a, b):
+            act(T.CP[0:16, 64 * a:64 * b], DD[0:16, 1024 + 64 * a:1024 + 64 * b], AF.Identity, ["D2"], keys("CPd", a, b))
+
+        def spread_pe(a, b):
+            mm(DD[:, 1536 + 64 * a:1536 + 64 * b], T.Ex[0:16, :], T.CP[0:16, 256 + 64 * a:256 + 64 * b], False, True, ["Ex"] + keys("CPa", a, b), ["D3"])
+            mm(T.M1[:, 256 + 64 * a:256 + 64 * b], T.Ex[0:16, :], T.CP[0:16, 64 * a:64 * b], True, True, ["Ex"] + keys("CPd", a, b), ["M1"])
+
+        def spread_v(a, b):
+            scan(T.SO[:, 64 * a:64 * b], T.rneg[:, 64 * a:64 * b], DD[:, 1536 + 64 * a:1536 + 64 * b], A.add, A.max, ["rneg", "D3"], keys("SO", a, b))
+
+        def spread_a(a, b):
+            act(T.RO[:, 64 * a:64 * b], T.M1[:, 256 + 64 * a:256 + 64 * b], AF.Identity, ["M1"], keys("RO", a, b))
+            lin(T.nb[:, 4 * a:4 * b], T.SO[:, 64 * a + 15:64 * b:16], -8192.0, 0.0, keys("SO", a, b), keys("nb", a, b))
+
+        def spread_mask(a, b):
+            mm(DD[:, 1536 + 64 * a:1536 + 64 * b], T.idb[:], T.nbig[:, 64 * a:64 * b], True, False, ["idb", "nbig"], ["D3"])
+
+        def differ(seg, on_vector):
+            k = seg // 4
+            o, src = T.EQ[:, 64 * seg:64 * seg + 64], T.RO[:, 64 * k:64 * k + 64]
+            if on_vector:
+                ts(o, src, T.SO[:, 16 * seg + 15:16 * seg + 16], 8192.0, A.not_equal, A.mult, ["RO%d" % k, "SO%d" % k], ["EQ%d" % seg])
+            else:
+                act(o, src, AF.Abs, ["RO%d" % k, "nb%d" % k], ["EQ%d" % seg], scale=8192.0, bias=T.nb[:, seg:seg + 1])
+
+        def first(a, b):
+            scan(T.SD[:, 256 * a:256 * b], T.EQ[:, 256 * a:256 * b], T.cm[:, 256 * a:256 * b], A.min, A.max,
+                 ["cm%d" % k for k in range(a, b)] + ["EQ%d" % j for j in range(4 * a, 4 * b)], ["SD%d" % k for k in range(a, b)])
+
+        def lists(a, b):
+            ks = range(a, b)
+            return [lambda: lists_a(a, b, ks), lambda: lists_b(a, b, ks), lambda: lists_c(a, b, ks)]
+
+        def lists_a(a, b, ks):
+            tt(T.to[:, 4 * a:4 * b], T.SO[:, 64 * a + 15:64 * b:16], T.SD[:, 256 * a + 63:256 * b:64], A.subtract,
+               keys("SO", a, b) + ["SD%d" % k for k in ks], ["to%d" % k for k in ks])
+
+        def lists_b(a, b, ks):
+            tt(T.tm[:, 4 * a:4 * b], T.to[:, 4 * a:4 * b], T.DU[:, 4 * a:4 * b], A.min, ["DU"] + ["to%d" % k for k in ks], ["tm%d" % k for k in ks])
+
+        def lists_c(a, b, ks):
+            ts(T.LO[:, 4 * a:4 * b], T.tm[:, 4 * a:4 * b], 8192.0, None, A.add, None, ["tm%d" % k for k in ks], ["LO%d" % k for k in ks])
+
+        def slow_a():
+            scan(T.SX[:], T.rmax[:], T.KF[:, 0:128], A.add, A.max, ["rmax", "KF"], ["SX"])
+
+        def slow_b():
+            cp(T.jt[:], T.SX[:, 15:128:16], ["SX"], ["jt"])
+
+        def slow_c():
+            ts(T.P6[:, 72:80], T.jt[:], 6, 63, A.logical_shift_right, A.bitwise_and, ["jt"], ["P6j"])
+
+        def slow_d():
+            cp(T.Pb[:, 72:80], T.P6[:, 72:80], ["P6j"], ["Pbj"])
+
+        def slow_e():
+            mm(T.KC[0:16, 0:64], T.Pb[:, 72:88], I2[1], True, True, ["Pbj", "Pbz", i2[1]], ["KC"])
+
+        def slow_f():
+            act(T.CP[0:16, 192:256], T.KC[0:16, 0:64], AF.Identity, ["KC"], ["CPj"])
+
+        def slow_g():
+            mm(T.KC[:, 64:192], T.Ex[0:16, :], T.CP[0:16, 192:320], True, True, ["Ex", "CPj", "CPa0"], ["KC"])
+
+        def col_a():
+            tt(T.d1[:], T.KC[:, 128:192], T.Fr[:], A.subtract, ["KC", "Fr"], ["d1"])
+
+        def col_b():
+            ts(T.oh[:], T.KC[:, 64:128], JC, None, A.is_equal, None, ["KC", "JC"], ["oh"])
+
+        def col_c():
+            tt(T.d2[:], T.d1[:], T.oh[:], A.mult, ["d1", "oh"], ["d2"])
+
+        def col_d():
+            tt(T.FW[:].indirect(T.LO[:, 8:12]), T.Fr[:], T.d2[:], A.add, ["Fr", "d2", "LO2"], ["FW", "FWd"])
+
+        new_words = [
+            lambda: tt(T.te[:], T.SO[:, 15:128:16], T.DU[:, 16:24], A.min, ["SO0", "SO1", "DUe"], ["te"]),
+            lambda: cp(T.LE[:], T.te[:], ["te"], ["LE"]),
+            lambda: tt(T.xs[:], T.X[:].indirect(T.LE[:, 0:4]), zc(64 * lam, 64 * lam + 64), A.add, ["X", "Xd", "LE", zk], ["xs"]),
+            lambda: ts(T.xl[:], T.X[:].indirect(T.LE[:, 4:8]), CD, 0.0, A.add, A.max, ["X", "Xd", "LE", "CD"], ["xl"]),
+            lambda: ts(T.xh[:], T.xs[:], C1, C2 if s == 0 else C3, A.mult, A.add, ["xs", "C1", "C2", "C3"], ["xh"]),
+            lambda: ts(T.xw[:], T.xh[:], CMX, None, A.min, None, ["xh", "CMX"], ["xw"])]
+
+        def put_l():
+            cp(T.X[:].indirect(T.LO[:, 4:8]), T.xl[:], ["xl", "LO1"], ["X", "Xd"])
+
+        def put_w():
+            cp(T.X[:].indirect(T.LO[:, 0:4]), T.xw[:], ["xw", "LO0"], ["X", "Xd"])
+
+        def dedupe(plan, segs):
+            nv = plan.count("e")
+            todo = list(segs[:nv])
+            for seg in segs[nv:]:
+                differ(seg, False)
+            for ch in plan:
+                if ch == "w":
+                    new_words.pop(0)()
+                elif ch == "e":
+                    differ(todo.pop(0), True)
+                elif ch == "a":
+                    col_a()
+                elif ch == "b":
+                    col_b()
+                elif ch == "c":
+                    col_c()
+
+        if not last:
+            place()
+            route()
+            ts(T.P6[:, 24:40], T.R[:, 0:16], 63, None, A.bitwise_and, None, ["Rw"], ["P6w"])
+            move_b()
+            cp(T.Pb[:, 8:40], T.P6[:, 8:40], ["P6w", "V1"], ["Pbw"])
+            move_q()
+            loser()
+            move_o()
+            move_p()
+            move_z()
+            order("g", [pk + "z", pk + "q"], [])
+            tr = []
+            sent = 0
+            for b, (dst, m, per) in enumerate(travel_engines(T, topo, rank, s)):
+                rid, pid = topo.addr(dst)[0], topo.addr(dst)[1]
+                tr.append(RemoteDMATransfer(dst_ids=[DstId(rid=rid, pnc=pid)], dma_engine_mask=m, remote_sem=T.sem["arr%d" % (s + 1)],
+                                            src=pay[:, 64 * b:64 * b + 64], dst=T["L%d" % (s + 1)][:, 64 * b:64 * b + 64]))
+                sent += per
+            g.remote_dma_fused(tr, local_sem=T.sem["sent%d" % s])
+            count["sent%d" % s] = sent
+            ts(T.P6[:, 40:56], T.R[:, 16:32], 63, None, A.bitwise_and, None, ["Rl"], ["P6l"])
+            flag_w()
+            flag_k()
+            cp(T.Pb[:, 40:72], T.P6[:, 40:72], ["P6l", "P6k", "P6h"], ["Pbl", "Pbk"])
+            if s == 0:
+                later_consts()
+                tt(T.Ex[0:16, :], T.E0[0:16, :], T.E8[0:16, :], A.add, ["E0", "E8"], ["Ex"])
+            spread_mask(0, 3)
+            compact(1, 0, 3)
+            compact(0, 0, 3)
+            copy_asc(0, 3)
+            copy_desc(0, 3)
+            slow_a()
+            slow_b()
+            slow_c()
+            slow_d()
+            spread_pe(0, 3)
+            spread_v(0, 3)
+            spread_a(0, 3)
+            slow_e()
+            slow_f()
+            slow_g()
+            dedupe(OPT["plan"], list(range(12)))
+            ls = lists(0, 3)
+            tail = [lambda: first(0, 3), col_a, ls[0], col_b, ls[1], col_c, ls[2], col_d, put_l, put_w]
+            while len(tail) > OPT["defer"]:
+                tail.pop(0)()
+            return tail
+        loser()
+        route()
+        ts(T.P6[:, 24:56], T.R[:], 63, None, A.bitwise_and, None, ["Rw", "Rl"], ["P6w", "P6l"])
+        flag_w()
+        cp(T.Pb[:, 24:72], T.P6[:, 24:72], ["P6w", "P6l", "P6k", "P6h"], ["Pbw", "Pbl", "Pbk"])
+        spread_mask(0, 2)
+        compact(1, 0, 2)
+        compact(0, 0, 2)
+        copy_asc(0, 2)
+        copy_desc(0, 2)
+        flag_k()
+        slow_a()
+        place()
+        slow_b()
+        spread_pe(0, 2)
+        spread_v(0, 2)
+        spread_a(0, 2)
+        slow_c()
+        compact(1, 2, 3)
+        compact(0, 2, 3)
+        dedupe(OPT["last_plan"], list(range(8)))
+        copy_asc(2, 3)
+        copy_desc(2, 3)
+        spread_mask(2, 3)
+        spread_pe(2, 3)
+        move_q()
+        first(0, 2)
+        lx, lf = lists(0, 2), lists(2, 3)
+        for call in (slow_d, lx[0], lambda: spread_v(2, 3), lx[1], slow_e, slow_f, slow_g, lx[2], lambda: spread_a(2, 3), put_l, put_w):
+            call()
+        dma("s", T.yx[:], T.X[:, 0:4096], ["X"], [])
+        for seg in range(8, 12):
+            differ(seg, False)
+        act(T.qout[0:8, :], T.M2[0:8, 0:128], AF.Identity, ["M2"], ["qout"])
+        dma("a", T.yq[:], T.qout[0:8, :], ["qout"], [])
+        for call in (move_b, lambda: first(2, 3), col_a, lf[0], col_b, lf[1], col_c, lf[2], move_o, col_d):
+            call()
+        dma("s", T.yf[:], T.FW[:, 0:512], ["FW"], [])
+        greatest()
+        move_z()
+        return []
+
+    rest = []
+    for s in range(STEPS):
+        rest = step(s, rest)
+
+    for sem, val in count.items():
+        g.wait_ge(T.sem[sem], val)

@@ -4,8 +4,8 @@ from concourse.mybir import dt, AluOpType, ActivationFunctionType
 N, STEPS, NB = 8, 3, 4
 BIG = 33554432.0
 F32, BF, I32, U16 = "float32", "bfloat16", "int32", "uint16"
-OPT = {"light": False, "shift": [1, 0, 0], "classes": 4, "cut": 96, "hib": 0, "kfirst": 0, "cm_early": False, "defer": 0,
-       "hash0": "hkhkhhhkhl", "hash": "hkhhhhh", "order0": "fcfcfclclc", "order": "fcfcfckckc", "plan": "wewewwewew", "last_plan": "wewewwww"}
+OPT = {"r1": 512, "loads": [("s", "z"), ("a", "h"), ("s", "a"), ("a", "q"), ("s", "s"), ("a", "f"), ("s", "x"), ("a", "t")], "ffirst": True, "a1": 0, "rs": [512, 512, 512], "rat": 1, "light": False, "shift": [1, 0, 0], "classes": 4, "cut": 96, "hib": 0, "kfirst": 1, "cm_early": False, "defer": 3,
+       "hash0": "lhlhlhhhkhkkll", "hash": "hkhlhhhh", "order0": "fcfcfclclc", "order": "hfhlfclfckckcc", "plan": "wewewwewew", "last_plan": "wewewwww"}
 
 
 def _s(cols, dtype, parts=128):
@@ -14,9 +14,9 @@ def _s(cols, dtype, parts=128):
 
 SCRATCH = {
     "X": _s(4160, BF), "FW": _s(576, F32), "fwi": _s(512, I32), "swi": _s(256, I32), "awi": _s(256, I32),
-    "Sp": _s(256, F32), "LP": _s(256, F32), "zin": _s(128, BF), "L1": _s(256, BF), "L2": _s(256, BF),
+    "awf": _s(256, F32), "Sp": _s(256, F32), "LP": _s(256, F32), "zin": _s(128, BF), "L1": _s(256, BF), "L2": _s(256, BF),
     "pay0": _s(256, BF), "pay1": _s(256, BF), "zout": _s(128, BF), "qout": _s(128, F32),
-    "hwi": _s(8, I32), "thi": _s(8, I32), "thr": _s(16, F32), "c1088": _s(16, BF), "onef": _s(128, F32),
+    "hwi": _s(128, I32), "hwb": _s(128, BF), "thi": _s(8, I32), "thr": _s(16, F32), "c1088": _s(16, BF), "onef": _s(128, F32),
     "qi": _s(128, I32), "qb": _s(256, I32), "qh": _s(256, BF),
     "pi": _s(8, I32), "pm": _s(8, I32), "col": _s(16, F32), "G8": _s(16, BF),
     "J16": _s(128, F32), "Jd": _s(16, F32), "vc": _s(256, F32),
@@ -162,14 +162,12 @@ def rank_program(g, core, T, topo):
     PM, HW, WT, ZB, ZS, C1, C2, CMX, CD, JC, P16, IS15, CB, C3 = [C[:, i:i + 1] for i in range(14)]
     DD = T.DD
 
-    dma("s", T.zin[:], T.z0[:], [], ["zin"])
-    dma("a", T.hwi[:, 0:1], T.hw[:], [], ["hwi"])
-    dma("s", T.awi[:], T.aw[:], [], ["awi"])
-    dma("a", T.qi[0:8, :], T.q0[:], [], ["qi"])
-    dma("s", T.swi[:], T.sw[:], [], ["swi"])
-    dma("a", T.fwi[:], T.fw[:], [], ["fwi"])
-    dma("s", T.X[:, 0:4096], T.lx[:], [], ["X"])
-    dma("a", T.thi[0:1, 0:8], T.th[:], [], ["thi"])
+    loads = {"z": (T.zin[:], T.z0[:], "zin"), "h": (T.hwi[0:1, :], T.hw[:], "hwi"), "a": (T.awi[:], T.aw[:], "awi"),
+             "q": (T.qi[0:8, :], T.q0[:], "qi"), "s": (T.swi[:], T.sw[:], "swi"), "f": (T.fwi[:], T.fw[:], "fwi"),
+             "x": (T.X[:, 0:4096], T.lx[:], "X"), "t": (T.thi[0:1, 0:8], T.th[:], "thi")}
+    for q, names_ in OPT["loads"]:
+        for ch in names_:
+            dma(q, loads[ch][0], loads[ch][1], [], [loads[ch][2]])
 
     ms(T.on[:], 1.0, ["on"])
     ms(T.c32[:], 32.0, ["c32"])
@@ -208,10 +206,9 @@ def rank_program(g, core, T, topo):
     ts(T.own[:, 0:128], T.J16[:], PM, None, A.is_equal, None, ["J16", "PM"], ["own0"])
     ts(T.rneg[:, 0:128], T.J16[:], 0.0, -BIG, A.is_equal, A.mult, ["J16"], ["rneg"])
     ts(T.ZO[:], T.J16[:, 0:16], 1.0, None, A.mult, None, ["J16"], ["ZO0"])
-    cp(HW, T.hwi[:, 0:1], ["hwi"], ["HW"])
-    ts(T.Hb[:], T.BM[:], HW, None, A.mult, None, ["BM", "HW"], ["Hb"])
-    ts(T.qb[0:8, 0:128], T.qi[0:8, :], 63, None, A.bitwise_and, None, ["qi"], ["qb0"])
-    ts(T.qb[0:8, 128:256], T.qi[0:8, :], 6, None, A.logical_shift_right, None, ["qi"], ["qb1"])
+    cp(T.hwb[0:1, :], T.hwi[0:1, :], ["hwi"], ["hwb"])
+    mm(T.KC[:, 0:2], T.hwb[0:1, :], T.on[0:1, 0:2], True, True, ["hwb", "on"], ["KC"])
+    ts(T.Hb[:], T.BM[:], T.KC[:, 0:1], None, A.mult, None, ["BM", "KC"], ["Hb"])
     lin(ZB, IS15, 15.0, 0.0, ["IS15"], ["ZB"])
     lin(WT, IS15, 61440.0, 4096.0, ["IS15"], ["WT"])
     lin(ZS, IS15, -1.0, 1.0, ["IS15"], ["ZS"])
@@ -279,9 +276,10 @@ def rank_program(g, core, T, topo):
         mm(T.M2[:, 128:136], zc(0, 128), T.Hb[:, 0:128:16], True, True, [zk, "Hb"], ["M2"])
         zall = ["zx%d" % c for c in range(4)]
 
-        def repeat(q, t0, t1):
+        def repeat(q, t0, t1, js):
             keys = ["zq%s%d" % (q, j) for j in range(5)]
-            for j, (o, st) in enumerate(((0, 16), (8, 16), (4, 8), (2, 4), (1, 2))):
+            for j in js:
+                o, st = ((0, 16), (8, 16), (4, 8), (2, 4), (1, 2))[j]
                 dst = T.zx[:, 16 * t0 + o:16 * t1:st]
                 src = zc(t0, t1) if j < 2 else T.zx[:, 16 * t0:16 * t1:st]
                 rd = [zk] if j < 2 else keys[:j]
@@ -298,23 +296,29 @@ def rank_program(g, core, T, topo):
         cut = 128 if s == 0 else OPT["cut"]
         if cut < 128:
             order("g", [], zall)
-        zx_keys = repeat("a", 0, cut) + (repeat("g", cut, 128) if cut < 128 else []) + zall
-        if s == 0:
-            cp(T.qh[0:8, :], T.qb[0:8, :], ["qb0", "qb1"], ["qh"])
-            ts(T.LP[:], T.awi[:], 3232.0, -6619136.0, A.mult, A.add, ["awi"], ["LP"])
+        a1 = OPT["a1"] if s > 0 else 0
+        zx_keys = repeat("a", 0, cut, range(4 if a1 == 1 else 5)) + (repeat("g", cut, 128, range(5)) if cut < 128 else []) + zall
         chain_h = [
             lambda: scan(T.SU[:], T.rneg[:, 0:128], T.M1[:, 0:128], A.add, A.max, ["rneg", "M1"], ["SU"]),
             lambda: cp(T.ui[:], T.SU[:, 15:128:16], ["SU"], ["ui"]),
             lambda: ts(T.hb[:, 16:24], T.ui[:], 2, 511, A.logical_shift_right, A.bitwise_and, ["ui"], ["hb2"]),
             lambda: ts(T.hb[:, 0:8], T.ui[:], 3, 255, A.logical_shift_right, A.bitwise_and, ["ui"], ["hb0"]),
             lambda: ts(T.hb[:, 8:16], T.ui[:], 255, None, A.bitwise_and, None, ["ui"], ["hb1"]),
-            lambda: cp(T.ho[:], T.hb[:], ["hb0", "hb1", "hb2"], ["ho"])]
+            lambda: cp(T.ho[:], T.hb[:], ["hb0", "hb1", "hb2"], ["ho", "hoF"])]
+        tail_h = []
+        if OPT["ffirst"] and s > 0:
+            tail_h = [chain_h[4], lambda: cp(T.ho[:, 0:16], T.hb[:, 0:16], ["hb0", "hb1"], ["ho"])]
+            chain_h = chain_h[0:4] + [lambda: cp(T.ho[:, 16:24], T.hb[:, 16:24], ["hb2"], ["hoF"]), lambda: None]
         chain_k = [
             lambda: cp(T.ut[:], T.M2[:, 128:136], ["M2"], ["ut"]),
             lambda: ts(T.P6[:, 56:64], T.ut[:], 2, 63, A.logical_shift_right, A.bitwise_and, ["ut"], ["P6k"]),
             lambda: ts(T.P6[:, 64:72], T.ut[:], 8, 7, A.logical_shift_right, A.bitwise_and, ["ut"], ["P6h"])]
         if s == 0:
-            late = [lambda: ts(T.Sp[:], T.swi[:], -2048.0, None, A.add, None, ["swi"], ["Sp"])]
+            late = [lambda: ts(T.qb[0:8, 0:128], T.qi[0:8, :], 63, None, A.bitwise_and, None, ["qi"], ["qb0"]),
+                    lambda: ts(T.qb[0:8, 128:256], T.qi[0:8, :], 6, None, A.logical_shift_right, None, ["qi"], ["qb1"]),
+                    lambda: cp(T.qh[0:8, :], T.qb[0:8, :], ["qb0", "qb1"], ["qh"]),
+                    lambda: ts(T.LP[:], T.awi[:], 3232.0, -6619136.0, A.mult, A.add, ["awi"], ["LP"]),
+                    lambda: ts(T.Sp[:], T.swi[:], -2048.0, None, A.add, None, ["swi"], ["Sp"])]
         for ch in (OPT["hash0"] if s == 0 else OPT["hash"]):
             if ch == "h":
                 chain_h.pop(0)()
@@ -322,6 +326,10 @@ def rank_program(g, core, T, topo):
                 chain_k.pop(0)()
             else:
                 fill()
+        if a1:
+            act(T.A1[:], T.awf[:].indirect(T.ho[:, 0:8]), AF.Identity, ["awf", "ho"], ["A1"], bias=32.0)
+            if a1 == 1:
+                repeat("a", 0, cut, [4])
         mm(T.M2[:, 0:128], T.idb[:], T.nbig[:, 0:128], True, False, ["idb", "nbig"], ["M2"])
         if s == 0:
             mm(T.M2[:, 0:128], T.E0[0:8, :], T.qh[0:8, 0:128], False, False, ["E0", "qh"], ["M2"])
@@ -330,10 +338,11 @@ def rank_program(g, core, T, topo):
             mm(T.M2[:, 0:128], T.Ex[0:16, :], Z[0:16, 1:256:2], False, True, ["Ex", zk], ["M2"])
         nF = 4 - OPT["shift"][s]
         for c in range(nF):
-            mm(DD[:, 512 * c:512 * c + 512], T.NI[:, 0:128], T.zx[:, 512 * c:512 * c + 512], True, False, ["NI0"] + zx_keys, ["D%d" % c])
+            mm(DD[:, 512 * c:512 * c + 512], T.NI[:, 0:128], T.zx[:, 512 * c:512 * c + 512], True, False,
+               ["NI0"] + (zx_keys[0:5] if 32 * c + 32 <= cut else zx_keys[0:10]) + zall, ["D%d" % c])
         Fw, fk = (T.fwi[:], "fwi") if s == 0 else (T.FW[:, 0:512], "FW")
         chain_f = [
-            lambda: tt(T.t1[:], Fw.indirect(T.ho[:, 16:24]), T.nown[:], A.mult, [fk, "ho", "nown"], ["t1"]),
+            lambda: tt(T.t1[:], Fw.indirect(T.ho[:, 16:24]), T.nown[:], A.mult, [fk, "hoF", "nown"], ["t1"]),
             lambda: tt(T.nf[:, 0:128], T.t1[:], T.M2[:, 0:128], A.max, ["t1", "M2"], ["nf0"]),
             lambda: cp(T.off[:, 0:128], T.nf[:, 0:128], ["nf0"], ["off0"])]
         chain_c = [
@@ -342,6 +351,8 @@ def rank_program(g, core, T, topo):
             lambda: tt(T.xi[:], T.LP[:].indirect(T.ho[:, 0:8]), T.pr[:], A.add, ["LP", "ho", "pr"], ["xi"]),
             lambda: ts(T.ci[:], T.xi[:], 5, 4095, A.arith_shift_right, A.bitwise_and, ["xi"], ["ci"]),
             lambda: cp(T.off[:, 128:256], T.ci[:], ["ci"], ["off1"])]
+        if a1:
+            chain_c[0] = lambda: None
         if s == 0:
             late = [lambda: ts(T.thr[0:1, 0:8], T.thi[0:1, 0:8], 4096.0, None, A.mult, None, ["thi"], ["THa"]),
                     lambda: ts(T.thr[0:1, 8:16], T.thi[0:1, 0:8], 4096.0, None, A.mult, None, ["thi"], ["THb"])]
@@ -350,6 +361,8 @@ def rank_program(g, core, T, topo):
                 chain_f.pop(0)()
             elif ch == "c":
                 chain_c.pop(0)()
+            elif ch == "h":
+                tail_h.pop(0)()
             elif ch == "k":
                 chain_k.pop(0)()
             else:
@@ -358,20 +371,15 @@ def rank_program(g, core, T, topo):
         cp(T.nf[:, 128:256], T.ci[:], ["ci"], ["nf1"])
         if s == 0:
             race_consts()
-            learn_consts_a()
-            if OPT["cm_early"]:
-                learn_consts_b()
-            cp(T.FW[:, 0:512], T.fwi[:], ["fwi"], ["FW"])
 
         def old_column():
-            act(T.Fr[:], T.FW[:, 0:512].indirect(T.ho[:, 16 + 4 * lam:20 + 4 * lam]), AF.Identity, ["FW", "ho"], ["Fr"])
+            act(T.Fr[:], T.FW[:, 0:512].indirect(T.ho[:, 16 + 4 * lam:20 + 4 * lam]), AF.Identity, ["FW", "hoF"], ["Fr"])
 
         def upper(r):
             act(T.hib[:, 128 * r:128 * r + 128], T.nf[:, 128 * r:128 * r + 128], AF.Identity, ["nf%d" % r], ["hib%d" % r], bias=12256.5)
 
-        if s > 0:
-            old_column()
-        upper(0)
+        if not OPT["ffirst"] or s == 0:
+            upper(0)
         VK = T.M1[:, 128:144]
         mm(VK, T.on[0:1, :], T.c1088[0:1, :], True, False, ["on", "c1088"], ["M1"])
         mm(VK, T.onef[0:1, :], T.thr[0:1, :], False, False, ["onef", "THa", "THb"], ["M1"])
@@ -383,8 +391,74 @@ def rank_program(g, core, T, topo):
             mm(VK, Z[0:16, 1:256:2], T.idb[0:16, 0:16], False, True, ["idb", zk], ["M1"])
 
         Xw = T.X[:, 0:4096]
+        P = slice(0, 64) if last else slice(0, 128)
+
+        def half_open(h, r):
+            K, k = (T.KC, "KC") if r else (T.KF, "KF")
+            o = K[64 * h:64 * h + 64, 256 * h:256 * h + 256]
+            t0 = 128 * r + 64 * h
+            mm(o, T.on[0:1, 0:64], T.CK[0:1, 256 * r:256 * r + 256], True, False, ["on", "CK%d" % r], [k])
+            mm(o, T.hib[:, t0:t0 + 64], T.NI[:], False, False, ["hib%d" % r, "NI0", "NI1"], [k])
+            mm(K[64 * h:64 * h + 64, 256 * h:256 * h + 128], T.nf[:, t0:t0 + 64], T.idf[:], False, False, ["nf%d" % r, "idf"], [k])
+
+        def half_keys(h, K, k, src, c0, b0, rd, stop, cls=range(16)):
+            for i in cls:
+                mm(K[64 * h:64 * h + 64, 256 * h + i:256 * h + 256:16], src[:, c0 + 1024 * h + i:c0 + 1024 * h + 1024:16], T.Bk[:, b0:b0 + 16],
+                   False, stop and i == 15, rd, [k])
+
+        def half_f(h):
+            for c in (2 * h, 2 * h + 1):
+                act(T.WF[:, 512 * c:512 * c + 512], Xw.indirect(T.off[:, 32 * c:32 * c + 32]), AF.Identity, ["X", "off0"], ["WF%d" % c])
+                mm(DD[:, 512 * c:512 * c + 512], T.idb[:], T.WF[:, 512 * c:512 * c + 512], False, True, ["idb", "WF%d" % c], ["D%d" % c])
+
+        def half_abs(h, c):
+            act(T.Dw[:, 1024 * h + c:1024 * h + 1024:2], DD[:, 1024 * h + c:1024 * h + 1024:2], AF.Abs, ["D%d" % (2 * h), "D%d" % (2 * h + 1)],
+                ["Dw0%d" % (2 * h + c)])
+
+        def half_c(h):
+            tt(T.Dw[:, 2048 + 1024 * h:3072 + 1024 * h], Xw.indirect(T.off[:, 128 + 64 * h:192 + 64 * h]), T.zx[:, 1024 * h:1024 * h + 1024],
+               A.subtract, ["X", "off1"] + zx_keys, ["Dw1" if h else "Dw10"])
+
+        def half_relu(h):
+            ts(T.RC[:, 1024 * h:1024 * h + 1024], T.Dw[:, 2048 + 1024 * h:3072 + 1024 * h], 0.0, None, A.max, None,
+               ["Dw1" if h else "Dw10"], ["RC" if h else "RCa"])
+
+        def half_race(h, now=True):
+            p = slice(64 * h, 64 * h + 64)
+            S1, K1, k1, S2, K2, k2 = (T.SC, T.KC, "C", T.SF, T.KF, "F") if h else (T.SF, T.KF, "F", T.SC, T.KC, "C")
+            calls = [
+                lambda: scan(S1[p, :], T.rmin[p, :], K1[p, 256 * h:256 * h + 256], A.add, A.min, ["rmin0", "rmin1", "K" + k1], ["S" + k1]),
+                lambda: tt(T.m1[p, :], S1[p, 15:256:16], T.M1[p, 128:144], A.min, ["S" + k1, "M1"], ["m1"]),
+                lambda: scan(S2[p, :], T.rmin[p, :], K2[p, 256 * h:256 * h + 256], A.add, A.min, ["rmin0", "rmin1", "K" + k2], ["S" + k2]),
+                lambda: tt(T.R[p, 0:16], S2[p, 15:256:16], T.m1[p, :], A.min, ["S" + k2, "m1"], ["Rw"])]
+            if now:
+                for j in (0, 2, 1, 3):
+                    calls[j]()
+            return calls
+
+        if last:
+            half_f(0)
+            act(T.hib[:], T.nf[:], AF.Identity, ["nf0", "nf1"], ["hib0", "hib1"], bias=12256.5)
+            half_c(0)
+            half_open(0, 0)
+            half_open(0, 1)
+            half_relu(0)
+            half_abs(0, 0)
+            half_abs(0, 1)
+            half_keys(0, T.KF, "KF", T.Dw, 0, 0, ["Dw00", "Bk"], False, range(0, 16, 2))
+            half_keys(0, T.KC, "KC", T.Dw, 2048, 32, ["Dw10", "Bkn"], False)
+            half_keys(0, T.KF, "KF", T.Dw, 0, 0, ["Dw01", "Bk"], True, range(1, 16, 2))
+            half_c(1)
+            half_keys(0, T.KC, "KC", T.RC, 0, 16, ["RCa", "Bk2"], True)
+            half_f(1)
+            act(T.Dw[:, 1024:1536], DD[:, 1024:1536], AF.Abs, ["D2"], ["Dw02"])
+            act(T.Dw[:, 1536:2048], DD[:, 1536:2048], AF.Abs, ["D3"], ["Dw03"])
+            act(T.RC[:, 1024:1024 + OPT["r1"]], T.Dw[:, 3072:3072 + OPT["r1"]], AF.Relu, ["Dw1"], ["RC"])
+            half_race(0)
+            nF = 0
         for r, K, k in ((1, T.KC, "KC"), (0, T.KF, "KF")):
-            mm(K[:, 0:256], T.on[0:1, :], T.CK[0:1, 256 * r:256 * r + 256], True, False, ["on", "CK%d" % r], [k])
+            if not last:
+                mm(K[:, 0:256], T.on[0:1, :], T.CK[0:1, 256 * r:256 * r + 256], True, False, ["on", "CK%d" % r], [k])
 
         def names(r, K, k):
             mm(K[:, 0:256], T.hib[:, 128 * r:128 * r + 128], T.NI[:], False, False, ["hib%d" % r, "NI0", "NI1"], [k])
@@ -393,14 +467,22 @@ def rank_program(g, core, T, topo):
         for c in range(nF):
             act(T.WF[:, 512 * c:512 * c + 512], Xw.indirect(T.off[:, 32 * c:32 * c + 32]), AF.Identity, ["X", "off0"], ["WF%d" % c])
             mm(DD[:, 512 * c:512 * c + 512], T.idb[:], T.WF[:, 512 * c:512 * c + 512], False, True, ["idb", "WF%d" % c], ["D%d" % c])
+            if OPT["ffirst"] and s > 0:
+                if c == nF - 1:
+                    act(T.hib[:], T.nf[:], AF.Identity, ["nf0", "nf1"], ["hib0", "hib1"], bias=12256.5)
+                    names(1, T.KC, "KC")
+                    names(0, T.KF, "KF")
+                continue
             if c == 0:
                 names(0, T.KF, "KF")
             if c == min(1, nF - 1):
                 upper(1)
-            if c == min(2, nF - 1):
+            if c == nF - 1:
                 names(1, T.KC, "KC")
         light = OPT["light"]
-        if light:
+        if last:
+            dw0 = ["Dw0%d" % c for c in range(4)] + ["Dw0s"]
+        elif light:
             for h in range(2):
                 tt(T.Dw[:, 2048 + 1024 * h:3072 + 1024 * h], Xw.indirect(T.off[:, 128 + 64 * h:192 + 64 * h]), T.zx[:, 1024 * h:1024 * h + 1024],
                    A.subtract, ["X", "off1"] + zx_keys, ["Dw1%d" % h] + (["Dw1"] if h else []))
@@ -424,21 +506,26 @@ def rank_program(g, core, T, topo):
                 tt(T.WF[:, 512 * nF:2048], Xw.indirect(T.off[:, 32 * nF:128]), T.zx[:, 512 * nF:2048], A.subtract,
                    ["X", "off0"] + zx_keys, ["WF%d" % c for c in range(nF, 4)])
                 act(T.Dw[:, 512 * nF:2048], T.WF[:, 512 * nF:2048], AF.Abs, ["WF%d" % j for j in range(nF, 4)], ["Dw0s"])
-            tt(T.Dw[:, 2048:4096], Xw.indirect(T.off[:, 128:256]), T.zx[:], A.subtract,
-               ["X", "off1"] + zx_keys, ["Dw1"])
-            if s == 0:
-                old_column()
+            rs = OPT["rs"][s]
+            if rs:
+                tt(T.Dw[:, 2048:2048 + rs], Xw.indirect(T.off[:, 128:128 + rs // 16]), T.zx[:, 0:rs], A.subtract,
+                   ["X", "off1"] + zx_keys, ["Dw10"])
+                act(T.RC[:, 0:rs], T.Dw[:, 2048:2048 + rs], AF.Relu, ["Dw10"], ["RCa"])
+            tt(T.Dw[:, 2048 + rs:4096], Xw.indirect(T.off[:, 128 + rs // 16:256]), T.zx[:, rs:2048], A.subtract,
+               ["X", "off1"] + zx_keys, ["Dw1"] + ([] if rs else ["Dw10"]))
             for i in range(16):
-                mm(T.KC[:, i:256:16], T.Dw[:, 2048 + i:4096:16], T.Bk[:, 32:48], False, False, ["Dw1", "Bkn"], ["KC"])
-            ts(T.RC[:], T.Dw[:, 2048:4096], 0.0, None, A.max, None, ["Dw1"], ["RC"])
+                mm(T.KC[:, i:256:16], T.Dw[:, 2048 + i:4096:16], T.Bk[:, 32:48], False, False, ["Dw1", "Dw10", "Bkn"], ["KC"])
+            ts(T.RC[:, rs:2048], T.Dw[:, 2048 + rs:4096], 0.0, None, A.max, None, ["Dw1"], ["RC"] + ([] if rs else ["RCa"]))
             nc = OPT["classes"]
             for c in range(nc):
                 act(T.Dw[:, c:512 * nF:nc], DD[:, c:512 * nF:nc], AF.Abs, ["D%d" % j for j in range(nF)], ["Dw0%d" % c])
+            if s > 0:
+                old_column()
             dw0 = ["Dw0%d" % c for c in range(nc)] + ["Dw0s"]
             for c in range(nc):
                 if c == OPT["kfirst"]:
                     for i in range(16):
-                        mm(T.KC[:, i:256:16], T.RC[:, i:2048:16], T.Bk[:, 16:32], False, i == 15, ["RC", "Bk2"], ["KC"])
+                        mm(T.KC[:, i:256:16], T.RC[:, i:2048:16], T.Bk[:, 16:32], False, i == 15, ["RC", "RCa", "Bk2"], ["KC"])
                 for i in range(c, 16, nc):
                     mm(T.KF[:, i:256:16], T.Dw[:, i:2048:16], T.Bk[:, 0:16], False, i == 15, ["Dw0%d" % c, "Bk", "Dw0s"], ["KF"])
 
@@ -447,20 +534,20 @@ def rank_program(g, core, T, topo):
 
         if not last:
             greatest()
-        scan(T.SC[:], T.rmin[:], T.KC[:, 0:256], A.add, A.min, ["rmin0", "rmin1", "KC"], ["SC"])
-        tt(T.m1[:], T.SC[:, 15:256:16], VK, A.min, ["SC", "M1"], ["m1"])
-        scan(T.SF[:], T.rmin[:], T.KF[:, 0:256], A.add, A.min, ["rmin0", "rmin1", "KF"], ["SF"])
-        tt(T.R[:, 0:16], T.SF[:, 15:256:16], T.m1[:], A.min, ["SF", "m1"], ["Rw"])
-        if s == 0 and not OPT["cm_early"]:
-            learn_consts_b()
-        if last:
+            scan(T.SC[:], T.rmin[:], T.KC[:, 0:256], A.add, A.min, ["rmin0", "rmin1", "KC"], ["SC"])
+            tt(T.m1[:], T.SC[:, 15:256:16], VK, A.min, ["SC", "M1"], ["m1"])
+            scan(T.SF[:], T.rmin[:], T.KF[:, 0:256], A.add, A.min, ["rmin0", "rmin1", "KF"], ["SF"])
+            tt(T.R[:, 0:16], T.SF[:, 15:256:16], T.m1[:], A.min, ["SF", "m1"], ["Rw"])
+        if s == 0:
+            learn_consts_a()
+        if s == 1:
             lin(T.id64[:], T.idb[:], 64.0, 0.0, ["idb"], ["id64"])
 
         pay = None if last else T["pay%d" % s]
         pk = "pay%d" % s
 
         def loser():
-            tt(T.R[:, 16:32], T.SF[:, 15:256:16], T.SC[:, 15:256:16], A.max, ["SF", "SC"], ["Rl"])
+            tt(T.R[P, 16:32], T.SF[P, 15:256:16], T.SC[P, 15:256:16], A.max, ["SF", "SC"], ["Rl"])
 
         def place():
             ts(T.P6[:, 0:8], T.R[:, 0:8], 6, 15, A.logical_shift_right, A.bitwise_and, ["Rw"], ["V0"])
@@ -488,7 +575,7 @@ def rank_program(g, core, T, topo):
             cp(T.zo[:], DD[:, 0:8], ["D0"], ["zo"])
 
         def move_z():
-            rd = dw0 + ["Dw1", "Dw2", "zo", "ZS"]
+            rd = dw0 + ["Dw1", "Dw10", "Dw2", "zo", "ZS"]
             if last:
                 act(T.zout[:], T.Dw[:].indirect(T.zo[:]), AF.Abs, rd, ["zout"], scale=ZS)
                 dma("a", T.yz[:], T.zout[:], ["zout"], [])
@@ -496,7 +583,8 @@ def rank_program(g, core, T, topo):
                 act(pay[:, 0:256:2], T.Dw[:].indirect(T.zo[:]), AF.Abs, rd + ["ZB"], [pk + "z"], scale=ZS, bias=ZB)
 
         i2 = ["I2%da" % lam, "I2%db" % lam]
-        I2 = [T.I2[:, 128 * lam:128 * lam + 64], T.I2[:, 128 * lam + 64:128 * lam + 128]]
+        I2 = [T.I2[P, 128 * lam:128 * lam + 64], T.I2[P, 128 * lam + 64:128 * lam + 128]]
+        J, jk, j0 = (T.M2, "M2", 256) if last else (T.KC, "KC", 0)
 
         def flag_w():
             ts(T.IV[:, 8:24], T.P6[:, 8:24], 2048.0, 128.0, A.is_ge, A.mult, ["V1"], ["IV"])
@@ -511,14 +599,18 @@ def rank_program(g, core, T, topo):
             c0, bank = (1024, "D2") if h == 0 else (512, "D1")
             for k in range(a, b):
                 o = DD[0:16, c0 + 64 * k:c0 + 64 * k + 64]
-                mm(o, T.Pb[:, 24 + 16 * k:40 + 16 * k], I2[h], True, False, [("Pbw", "Pbl", "Pbk")[k], i2[h]], [bank])
+                mm(o, T.Pb[P, 24 + 16 * k:40 + 16 * k], I2[h], True, False, [("Pbw", "Pbl", "Pbk")[k], i2[h]], [bank])
                 if k < 2:
-                    mm(o, T.IV[:, 0:16], I2[h], False, True, ["IV", "IVz", i2[h]], [bank])
+                    mm(o, T.IV[P, 0:16], I2[h], False, True, ["IV", "IVz", i2[h]], [bank])
                 else:
-                    mm(o, T.IK[:], I2[h], False, True, ["IK", "IKz", i2[h]], [bank])
+                    mm(o, T.IK[P, :], I2[h], False, True, ["IK", "IKz", i2[h]], [bank])
 
-        def copy_asc(a, b):
-            act(T.CP[0:16, 256 + 64 * a:256 + 64 * b], DD[0:16, 512 + 64 * a:512 + 64 * b], AF.Identity, ["D1"], keys("CPa", a, b))
+        def copy_asc(a, b, on_vector=False):
+            o, src = T.CP[0:16, 256 + 64 * a:256 + 64 * b], DD[0:16, 512 + 64 * a:512 + 64 * b]
+            if on_vector:
+                cp(o, src, ["D1"], keys("CPa", a, b))
+            else:
+                act(o, src, AF.Identity, ["D1"], keys("CPa", a, b))
 
         def copy_desc(a, b):
             act(T.CP[0:16, 64 * a:64 * b], DD[0:16, 1024 + 64 * a:1024 + 64 * b], AF.Identity, ["D2"], keys("CPd", a, b))
@@ -564,7 +656,7 @@ def rank_program(g, core, T, topo):
             ts(T.LO[:, 4 * a:4 * b], T.tm[:, 4 * a:4 * b], 8192.0, None, A.add, None, ["tm%d" % k for k in ks], ["LO%d" % k for k in ks])
 
         def slow_a():
-            scan(T.SX[:], T.rmax[:], T.KF[:, 0:128], A.add, A.max, ["rmax", "KF"], ["SX"])
+            scan(T.SX[P, :], T.rmax[P, :], T.KF[P, 0:128], A.add, A.max, ["rmax", "KF"], ["SX"])
 
         def slow_b():
             cp(T.jt[:], T.SX[:, 15:128:16], ["SX"], ["jt"])
@@ -576,19 +668,19 @@ def rank_program(g, core, T, topo):
             cp(T.Pb[:, 72:80], T.P6[:, 72:80], ["P6j"], ["Pbj"])
 
         def slow_e():
-            mm(T.KC[0:16, 0:64], T.Pb[:, 72:88], I2[1], True, True, ["Pbj", "Pbz", i2[1]], ["KC"])
+            mm(J[0:16, j0:j0 + 64], T.Pb[P, 72:88], I2[1], True, True, ["Pbj", "Pbz", i2[1]], [jk])
 
         def slow_f():
-            act(T.CP[0:16, 192:256], T.KC[0:16, 0:64], AF.Identity, ["KC"], ["CPj"])
+            act(T.CP[0:16, 192:256], J[0:16, j0:j0 + 64], AF.Identity, [jk], ["CPj"])
 
         def slow_g():
-            mm(T.KC[:, 64:192], T.Ex[0:16, :], T.CP[0:16, 192:320], True, True, ["Ex", "CPj", "CPa0"], ["KC"])
+            mm(J[:, j0 + 64:j0 + 192], T.Ex[0:16, :], T.CP[0:16, 192:320], True, True, ["Ex", "CPj", "CPa0"], [jk])
 
         def col_a():
-            tt(T.d1[:], T.KC[:, 128:192], T.Fr[:], A.subtract, ["KC", "Fr"], ["d1"])
+            tt(T.d1[:], J[:, j0 + 128:j0 + 192], T.Fr[:], A.subtract, [jk, "Fr"], ["d1"])
 
         def col_b():
-            ts(T.oh[:], T.KC[:, 64:128], JC, None, A.is_equal, None, ["KC", "JC"], ["oh"])
+            ts(T.oh[:], J[:, j0 + 64:j0 + 128], JC, None, A.is_equal, None, [jk, "JC"], ["oh"])
 
         def col_c():
             tt(T.d2[:], T.d1[:], T.oh[:], A.mult, ["d1", "oh"], ["d2"])
@@ -655,18 +747,22 @@ def rank_program(g, core, T, topo):
             if s == 0:
                 later_consts()
                 tt(T.Ex[0:16, :], T.E0[0:16, :], T.E8[0:16, :], A.add, ["E0", "E8"], ["Ex"])
+                learn_consts_b()
             spread_mask(0, 3)
             compact(1, 0, 3)
             compact(0, 0, 3)
-            copy_asc(0, 3)
-            copy_desc(0, 3)
             slow_a()
+            copy_asc(0, 3, True)
+            copy_desc(0, 3)
             slow_b()
-            slow_c()
-            slow_d()
             spread_pe(0, 3)
+            slow_c()
             spread_v(0, 3)
+            slow_d()
             spread_a(0, 3)
+            if s == 0:
+                cp(T.FW[:, 0:512], T.fwi[:], ["fwi"], ["FW"])
+                old_column()
             slow_e()
             slow_f()
             slow_g()
@@ -684,11 +780,12 @@ def rank_program(g, core, T, topo):
         spread_mask(0, 2)
         compact(1, 0, 2)
         compact(0, 0, 2)
-        copy_asc(0, 2)
-        copy_desc(0, 2)
         flag_k()
         slow_a()
-        place()
+        if OPT["r1"] < 1024:
+            ts(T.RC[:, 1024 + OPT["r1"]:2048], T.Dw[:, 3072 + OPT["r1"]:4096], 0.0, None, A.max, None, ["Dw1"], ["RCb"])
+        copy_asc(0, 2, True)
+        copy_desc(0, 2)
         slow_b()
         spread_pe(0, 2)
         spread_v(0, 2)
@@ -696,26 +793,36 @@ def rank_program(g, core, T, topo):
         slow_c()
         compact(1, 2, 3)
         compact(0, 2, 3)
+        half_open(1, 1)
+        half_keys(1, T.KC, "KC", T.Dw, 2048, 32, ["Dw1", "Bkn"], False)
         dedupe(OPT["last_plan"], list(range(8)))
         copy_asc(2, 3)
         copy_desc(2, 3)
         spread_mask(2, 3)
         spread_pe(2, 3)
-        move_q()
         first(0, 2)
         lx, lf = lists(0, 2), lists(2, 3)
+        half_keys(1, T.KC, "KC", T.RC, 0, 16, ["RC", "RCb", "Bk2"], True)
+        old_column()
         for call in (slow_d, lx[0], lambda: spread_v(2, 3), lx[1], slow_e, slow_f, slow_g, lx[2], lambda: spread_a(2, 3), put_l, put_w):
             call()
+        half_open(1, 0)
+        half_keys(1, T.KF, "KF", T.Dw, 0, 0, ["Dw02", "Dw03", "Bk"], True)
         dma("s", T.yx[:], T.X[:, 0:4096], ["X"], [])
         for seg in range(8, 12):
             differ(seg, False)
-        act(T.qout[0:8, :], T.M2[0:8, 0:128], AF.Identity, ["M2"], ["qout"])
-        dma("a", T.yq[:], T.qout[0:8, :], ["qout"], [])
-        for call in (move_b, lambda: first(2, 3), col_a, lf[0], col_b, lf[1], col_c, lf[2], move_o, col_d):
+        hr = half_race(1, False)
+        for call in (hr[0], lambda: first(2, 3), hr[1], col_a, hr[2], lf[0], hr[3], col_b, lf[1], place, route, col_c, lf[2], move_b, col_d):
             call()
         dma("s", T.yf[:], T.FW[:, 0:512], ["FW"], [])
+        ts(T.P6[:, 24:40], T.R[:, 0:16], 63, None, A.bitwise_and, None, ["Rw"], ["P6w"])
         greatest()
+        cp(T.Pb[:, 24:40], T.P6[:, 24:40], ["P6w"], ["Pbw"])
+        move_q()
+        move_o()
         move_z()
+        act(T.qout[0:8, :], T.M2[0:8, 0:128], AF.Identity, ["M2"], ["qout"])
+        dma("s", T.yq[:], T.qout[0:8, :], ["qout"], [])
         return []
 
     rest = []

from concourse.bass import DstId, RemoteDMATransfer
from concourse.mybir import dt, AluOpType, ActivationFunctionType

N, STEPS, NB = 8, 3, 4
BIG = 33554432.0
F32, BF, I32, U16 = "float32", "bfloat16", "int32", "uint16"
OPT = {"r1": 512, "loads": [("s", "z"), ("a", "h"), ("s", "a"), ("a", "q"), ("s", "s"), ("a", "f"), ("s", "x"), ("a", "t")], "ffirst": True, "a1": 0, "rs": [512, 512, 512], "rat": 1, "light": False, "shift": [1, 0, 0], "classes": 4, "cut": 96, "hib": 0, "kfirst": 1, "cm_early": False, "defer": 3,
       "hash0": "lhlhlhhhkhkkll", "hash": "hkhlhhhh", "order0": "fcfcfclclc", "order": "hfhlfclfckckcc", "plan": "wewewwewew", "last_plan": "wewewwww"}


def _s(cols, dtype, parts=128):
    return ("sbuf", [parts, cols], dtype)


SCRATCH = {
    "X": _s(4160, BF), "FW": _s(576, F32), "fwi": _s(512, I32), "swi": _s(256, I32), "awi": _s(256, I32),
    "awf": _s(256, F32), "Sp": _s(256, F32), "LP": _s(256, F32), "zin": _s(128, BF), "L1": _s(256, BF), "L2": _s(256, BF),
    "pay0": _s(256, BF), "pay1": _s(256, BF), "zout": _s(128, BF), "qout": _s(128, F32),
    "hwi": _s(128, I32), "hwb": _s(128, BF), "thi": _s(8, I32), "thr": _s(16, F32), "c1088": _s(16, BF), "onef": _s(128, F32),
    "qi": _s(128, I32), "qb": _s(256, I32), "qh": _s(256, BF),
    "pi": _s(8, I32), "pm": _s(8, I32), "col": _s(16, F32), "G8": _s(16, BF),
    "J16": _s(128, F32), "Jd": _s(16, F32), "vc": _s(256, F32),
    "BM": _s(128, BF), "Hb": _s(128, BF), "SU": _s(128, F32), "SO": _s(192, F32), "rneg": _s(192, F32),
    "Bk": _s(48, BF), "own": _s(256, BF), "nown": _s(128, F32), "nbig": _s(192, BF), "o16": _s(128, BF),
    "idf": _s(128, F32), "idb": _s(128, BF), "id64": _s(128, BF), "NI": _s(256, BF), "E0": _s(128, BF), "E8": _s(128, BF), "Ex": _s(128, BF),
    "E64": _s(128, BF), "I8": _s(16, BF), "I2": _s(256, BF), "rmin": _s(256, F32), "rmax": _s(128, F32), "rM": _s(2048, BF),
    "ZO": _s(16, U16), "CK": _s(512, BF), "on": _s(128, BF), "s64": _s(128, BF), "c32": _s(128, BF), "cm": _s(768, BF), "DU": _s(24, F32),
    "ui": _s(8, I32), "hb": _s(24, I32), "ho": _s(24, U16), "A1": _s(128, F32), "pr": _s(128, F32), "xi": _s(128, I32),
    "ci": _s(128, I32), "t1": _s(128, F32), "nf": _s(256, F32), "hib": _s(256, BF), "off": _s(256, U16),
    "zx": _s(2048, BF), "WF": _s(2048, BF), "RC": _s(2048, BF), "Dw": _s(6144, BF), "Fr": _s(64, F32),
    "SF": _s(256, F32), "SC": _s(256, F32), "SX": _s(128, F32), "m1": _s(16, F32), "R": _s(32, I32),
    "E": _s(256, BF), "zo": _s(8, U16), "ut": _s(8, I32), "jt": _s(8, I32), "P6": _s(80, I32), "Pb": _s(88, BF),
    "te": _s(8, F32), "LE": _s(8, U16),
    "IV": _s(24, BF), "IK": _s(16, BF), "CP": _s(448, BF), "RO": _s(192, F32), "nb": _s(16, F32), "EQ": _s(768, BF), "SD": _s(768, BF),
    "to": _s(16, F32), "tm": _s(16, F32), "LO": _s(16, U16), "xl": _s(64, BF), "xs": _s(64, F32), "xh": _s(64, I32), "xw": _s(64, BF),
    "d1": _s(64, F32), "oh": _s(64, F32), "d2": _s(64, F32),
    "DD": ("psum", [128, 2048], F32),
    "KF": ("psum", [128, 512], F32), "KC": ("psum", [128, 512], F32), "M1": ("psum", [128, 512], F32), "M2": ("psum", [128, 512], F32),
}
BANKS = ("D0", "D1", "D2", "D3", "KF", "KC", "M1", "M2")
NDMA = 14
SEMAPHORES = ["qv", "qa", "qp", "qg", "arr1", "arr2", "sent0", "sent1"] + ["d%d" % i for i in range(NDMA)]


def travel_engines(T, topo, rank, s):
    src = T.cores[rank]
    dsts = [T.cores[(rank + 1 + b + s) % N] for b in range(NB)]
    common = [e for e in topo.engines(src, dsts[0]) if all(e in topo.engines(src, d) for d in dsts)]
    per = 1
    while 2 * per * NB <= len(common):
        per *= 2
    out = []
    for b in range(NB):
        m = 0
        for e in common[b * per:(b + 1) * per]:
            m |= 1 << e
        out.append((dsts[b], m, per))
    return out


def rank_program(g, core, T, topo):
    rank = T.rank_of(core)
    if rank is None:
        return
    A, AF = AluOpType, ActivationFunctionType
    Q = {"v": g.vector, "a": g.scalar, "p": g.tensor, "g": g, "s": g.sync}
    QS = {"v": "qv", "a": "qa", "p": "qp", "g": "qg"}
    count = {}
    known = {q: {} for q in Q}
    lastw, readers = {}, {}
    ndma = [0]

    def wait(q, tok):
        sem, val, clock = tok[0], tok[1], tok[2]
        if known[q].get(sem, 0) >= val:
            return
        Q[q].wait_ge(T.sem[sem], val)
        known[q][sem] = val
        for k, v in clock.items():
            if known[q].get(k, 0) < v:
                known[q][k] = v

    def order(q, r, w):
        deps = []
        for k in r:
            if k in lastw:
                deps.append(lastw[k])
            if k in BANKS:
                deps += [t for t in readers.get(k, []) if t[3] != q]
        for k in w:
            if k in lastw and not (k in BANKS and q == "p" and lastw[k][3] == "p"):
                deps.append(lastw[k])
            deps += readers.get(k, [])
        deps.sort(key=lambda t: -t[1])
        for t in deps:
            wait(q, t)

    def note(tok, r, w):
        for k in r:
            readers.setdefault(k, []).append(tok)
        for k in w:
            lastw[k] = tok
            readers[k] = []

    def op(q, call, r, w):
        order(q, r, w)
        sem = QS[q]
        count[sem] = count.get(sem, 0) + 1
        call().then_inc(T.sem[sem], 1)
        note((sem, count[sem], dict(known[q]), q), r, w)

    def dma(q, out, in_, r, w):
        order(q, r, w)
        sem = "d%d" % ndma[0]
        ndma[0] += 1
        count[sem] = 16
        Q[q].dma_start(out, in_).then_inc(T.sem[sem], 16)
        note((sem, 16, dict(known[q]), "dma"), r, w)

    V_ = g.vector

    def ts(out, in0, s1, s2, o0, o1, r, w):
        if o1 is None:
            op("v", lambda: V_.tensor_scalar(out, in0, s1, None, o0), r, w)
        else:
            op("v", lambda: V_.tensor_scalar(out, in0, s1, s2, o0, o1), r, w)

    def tt(out, in0, in1, o, r, w):
        op("v", lambda: V_.tensor_tensor(out, in0, in1, o), r, w)

    def cp(out, in_, r, w):
        op("v", lambda: V_.tensor_copy(out, in_), r, w)

    def ms(ap, c, w):
        op("v", lambda: V_.memset(ap, c), [], w)

    def scan(out, d0, d1, o0, o1, r, w):
        op("v", lambda: V_.tensor_tensor_scan(out, d0, d1, 0.0, o0, o1), r, w)

    def act(out, in_, f, r, w, **kw):
        op("a", lambda: g.scalar.activation(out, in_, f, **kw), r, w)

    def lin(out, in_, scale, bias, r, w):
        act(out, in_, AF.Identity, r, w, scale=scale, bias=bias)

    def mm(out, lhsT, rhs, start, stop, r, w):
        op("p", lambda: g.tensor.matmul(out, lhsT, rhs, start, stop), r, w)

    def iota(out, pat, base, cm, w, flag=True):
        if flag:
            op("g", lambda: g.iota(out, pat, base, cm, allow_small_or_imprecise_dtypes=True), [], w)
        else:
            op("g", lambda: g.iota(out, pat, base, cm), [], w)

    def sel(out, in_, pat, cmp, base, cm, r, w):
        op("g", lambda: g.affine_select(out, in_, pat, cmp, 0.0, base, cm), r, w)

    def zero(out, n, w):
        iota(out, [[0, n]], 0, 0, w)

    C = T.col
    PM, HW, WT, ZB, ZS, C1, C2, CMX, CD, JC, P16, IS15, CB, C3 = [C[:, i:i + 1] for i in range(14)]
    DD = T.DD

    loads = {"z": (T.zin[:], T.z0[:], "zin"), "h": (T.hwi[0:1, :], T.hw[:], "hwi"), "a": (T.awi[:], T.aw[:], "awi"),
             "q": (T.qi[0:8, :], T.q0[:], "qi"), "s": (T.swi[:], T.sw[:], "swi"), "f": (T.fwi[:], T.fw[:], "fwi"),
             "x": (T.X[:, 0:4096], T.lx[:], "X"), "t": (T.thi[0:1, 0:8], T.th[:], "thi")}
    for q, names_ in OPT["loads"]:
        for ch in names_:
            dma(q, loads[ch][0], loads[ch][1], [], [loads[ch][2]])

    ms(T.on[:], 1.0, ["on"])
    ms(T.c32[:], 32.0, ["c32"])
    ms(T.s64[0:16, :], 64.0, ["s64"])
    iota(T.pi[:, 0:1], [[0, 1]], 0, 1, ["pi"], False)
    iota(T.J16[:], [[0, 8], [1, 16]], 0, 0, ["J16"])
    sel(T.BM[:], T.on[:], [[-16, 8], [0, 16]], A.is_ge, 0, 1, ["on"], ["BM"])
    sel(T.BM[:], T.BM[:], [[16, 8], [0, 16]], A.is_ge, 15, -1, ["BM"], ["BM"])
    sel(T.idb[:], T.on[:], [[-1, 128]], A.is_equal, 0, 1, ["on"], ["idb"])
    sel(T.E0[0:16, :], T.on[0:16, :], [[-1, 8], [0, 16]], A.is_equal, 0, 1, ["on"], ["E0"])
    sel(T.E64[0:8, :], T.s64[0:8, :], [[-1, 8], [0, 16]], A.is_equal, 0, 1, ["s64"], ["E64"])
    sel(T.I8[0:8, :], T.on[0:8, 0:16], [[-1, 16]], A.is_equal, 8, 1, ["on"], ["I8"])
    iota(P16, [[0, 1]], 0, 16, ["P16"])
    iota(T.CK[0:1, 256:512], [[-12480, 2], [0, 8], [64, 16]], 12288 + 1024, 0, ["CK1"])
    iota(T.CK[0:1, 0:256], [[-12480, 2], [0, 8], [64, 16]], 12288, 0, ["CK0"])
    iota(T.vc[:], [[16, 4], [1, 64]], -63, 0, ["vc"])
    iota(T.Jd[:, 0:8], [[0, 2], [16, 4]], 4096 - 8192, 0, ["Jda"])
    iota(T.Jd[:, 8:12], [[16, 4]], 512 - 8192, 0, ["Jdb"])
    iota(T.rM[:], [[0, 128], [2048, 16]], -1024, 0, ["rM"])
    zero(T.pay0[:], 256, ["pay0z", "pay0q"])
    sel(T.E8[0:16, :], T.s64[0:16, :], [[-1, 8], [0, 16]], A.is_equal, -8, 1, ["s64"], ["E8"])
    sel(T.I2[:, 0:64], T.on[:, 0:64], [[1, 64]], A.is_equal, -63, 1, ["on"], ["I20a"])
    sel(T.I2[:, 64:128], T.on[:, 0:64], [[-1, 64]], A.is_equal, 0, 1, ["on"], ["I20b"])
    zero(T.IV[:, 0:8], 8, ["IVz"])
    zero(T.IK[:, 0:8], 8, ["IKz"])
    zero(T.Pb[:, 80:88], 8, ["Pbz"])
    zero(T.X[:, 4096:4160], 64, ["Xd"])
    zero(T.FW[:, 512:576], 64, ["FWd"])

    ts(T.pm[:, 0:1], T.pi[:, 0:1], 15, None, A.bitwise_and, None, ["pi"], ["pm"])
    ms(T.onef[0:1, :], 1.0, ["onef"])
    cp(PM, T.pm[:, 0:1], ["pm"], ["PM"])
    ms(T.c1088[0:1, :], -1088.0, ["c1088"])
    ts(IS15, PM, 15.0, None, A.is_equal, None, ["PM"], ["IS15"])
    ts(T.nown[:], T.J16[:], PM, None, A.not_equal, None, ["J16", "PM"], ["nown"])
    ts(T.own[:, 0:128], T.J16[:], PM, None, A.is_equal, None, ["J16", "PM"], ["own0"])
    ts(T.rneg[:, 0:128], T.J16[:], 0.0, -BIG, A.is_equal, A.mult, ["J16"], ["rneg"])
    ts(T.ZO[:], T.J16[:, 0:16], 1.0, None, A.mult, None, ["J16"], ["ZO0"])
    cp(T.hwb[0:1, :], T.hwi[0:1, :], ["hwi"], ["hwb"])
    mm(T.KC[:, 0:2], T.hwb[0:1, :], T.on[0:1, 0:2], True, True, ["hwb", "on"], ["KC"])
    ts(T.Hb[:], T.BM[:], T.KC[:, 0:1], None, A.mult, None, ["BM", "KC"], ["Hb"])
    lin(ZB, IS15, 15.0, 0.0, ["IS15"], ["ZB"])
    lin(WT, IS15, 61440.0, 4096.0, ["IS15"], ["WT"])
    lin(ZS, IS15, -1.0, 1.0, ["IS15"], ["ZS"])
    lin(T.nbig[:, 0:128], T.nown[:], -1048576.0, 0.0, ["nown"], ["nbig"])
    lin(T.NI[:, 0:128], T.idb[:], -1.0, 0.0, ["idb"], ["NI0"])

    def race_consts():
        lin(T.NI[:, 128:256], T.idb[:], 1.0 / 64, 0.0, ["idb"], ["NI1"])
        lin(T.idf[:], T.idb[:], 1.0, 0.0, ["idb"], ["idf"])
        lin(T.Bk[:, 0:8], T.BM[:, 0:128:16], WT, 0.0, ["BM", "WT"], ["Bk"])
        lin(T.Bk[:, 8:16], T.BM[:, 0:128:16], WT, 0.0, ["BM", "WT", "Bk"], ["Bk"])
        act(T.rmin[:, 0:128], T.J16[:], AF.Relu, ["J16"], ["rmin0"], scale=-BIG, bias=BIG)
        lin(T.Bk[:, 16:32], T.Bk[:, 0:16], 2.0, 0.0, ["Bk"], ["Bk2"])
        lin(T.Bk[:, 32:48], T.Bk[:, 0:16], -1.0, 0.0, ["Bk"], ["Bkn"])
        act(T.rmin[:, 128:256], T.J16[:], AF.Relu, ["J16"], ["rmin1"], scale=-BIG, bias=BIG)
        lin(T.own[:, 128:256], T.own[:, 0:128], 1.0, 0.0, ["own0"], ["own1"])
        lin(T.G8[:, 0:8], T.BM[:, 0:128:16], 1.0, 0.0, ["BM"], ["G8a"])
        lin(T.G8[:, 8:16], T.BM[:, 0:128:16], 2.0, 0.0, ["BM"], ["G8b"])
        lin(T.o16[:], T.own[:, 0:128], P16, 0.0, ["own0", "P16"], ["o16"])

    def learn_consts_a():
        lin(T.rmax[:], T.rmin[:, 0:128], -1.0, 128.0, ["rmin0"], ["rmax"])
        lin(CB, PM, -8192.0, 8192.0, ["PM"], ["CB"])
        lin(T.nbig[:, 128:192], T.nown[:, 0:64], -1048576.0, 0.0, ["nown", "nbig"], ["nbig"])
        lin(T.rneg[:, 128:192], T.rmin[:, 0:64], -1.0, 0.0, ["rmin0", "rneg"], ["rneg"])
        lin(T.DU[:, 0:12], T.Jd[:, 0:12], 1.0, PM, ["Jda", "Jdb", "PM"], ["DU"])
        lin(JC, PM, -1.0, 30.0, ["PM"], ["JC"])
        lin(T.DU[:, 16:24], T.DU[:, 0:8], 1.0, 8192.0, ["DU"], ["DUe"])
        lin(CD, IS15, -1.0, 0.0, ["IS15"], ["CD"])
        lin(C1, IS15, 0.5, 0.5, ["IS15"], ["C1"])
        lin(C2, IS15, 2.25, -0.25, ["IS15"], ["C2"])
        lin(C3, IS15, -12.75, -0.25, ["IS15"], ["C3"])
        lin(CMX, IS15, -240.0, 255.0, ["IS15"], ["CMX"])

    def learn_consts_b():
        for k in range(3):
            act(T.cm[:, 256 * k:256 * k + 256], T.vc[:], AF.Relu, ["vc", "CB"], ["cm%d" % k], scale=-8192.0, bias=CB)

    def later_consts():
        sel(T.I2[:, 128:192], T.on[:, 0:64], [[1, 64]], A.is_equal, -127, 1, ["on"], ["I21a"])
        sel(T.I2[:, 192:256], T.on[:, 0:64], [[-1, 64]], A.is_equal, -64, 1, ["on"], ["I21b"])
        zero(T.pay1[:], 256, ["pay1z", "pay1q"])

    def step(s, late):
        def fill(n=1):
            for _ in range(n):
                if late:
                    late.pop(0)()

        lam = s % 2
        last = s == STEPS - 1
        if s == 0:
            zk, Z, zs, zob, zok = "zin", T.zin, 1, 0, "ZO0"
        else:
            zk, Z, zs, zob, zok = "L%d" % s, T["L%d" % s], 2, 128, "ZO1"
            got = sum(m[2] for r2 in range(N) for m in travel_engines(T, topo, r2, s - 1) if m[0] == core)
            count["arr%d" % s] = got
            note(("arr%d" % s, got, {}, "remote"), [], [zk])

        def zc(a, b, step=1):
            return Z[:, zs * a:zs * b:zs * step]

        mm(T.M1[:, 0:128], T.idb[:], T.nbig[:, 0:128], True, False, ["idb", "nbig"], ["M1"])
        mm(T.M1[:, 0:128], T.Hb[:], zc(0, 128), False, True, [zk, "Hb"], ["M1"])
        mm(T.M2[:, 128:136], zc(0, 128), T.Hb[:, 0:128:16], True, True, [zk, "Hb"], ["M2"])
        zall = ["zx%d" % c for c in range(4)]

        def repeat(q, t0, t1, js):
            keys = ["zq%s%d" % (q, j) for j in range(5)]
            for j in js:
                o, st = ((0, 16), (8, 16), (4, 8), (2, 4), (1, 2))[j]
                dst = T.zx[:, 16 * t0 + o:16 * t1:st]
                src = zc(t0, t1) if j < 2 else T.zx[:, 16 * t0:16 * t1:st]
                rd = [zk] if j < 2 else keys[:j]
                wr = [keys[j]] + (zall if j == 0 else [])
                if q == "g":
                    n = (t1 - t0) * 16 // st
                    op("g", lambda: g.affine_select(dst, src, [[0, n]], A.is_ge, 0.0, 0, 0), rd, [keys[j]])
                elif s == 0 and j < 2:
                    act(dst, src, AF.Identity, rd + ["ZB"], wr, bias=ZB)
                else:
                    act(dst, src, AF.Identity, rd, wr)
            return keys

        cut = 128 if s == 0 else OPT["cut"]
        if cut < 128:
            order("g", [], zall)
        a1 = OPT["a1"] if s > 0 else 0
        zx_keys = repeat("a", 0, cut, range(4 if a1 == 1 else 5)) + (repeat("g", cut, 128, range(5)) if cut < 128 else []) + zall
        chain_h = [
            lambda: scan(T.SU[:], T.rneg[:, 0:128], T.M1[:, 0:128], A.add, A.max, ["rneg", "M1"], ["SU"]),
            lambda: cp(T.ui[:], T.SU[:, 15:128:16], ["SU"], ["ui"]),
            lambda: ts(T.hb[:, 16:24], T.ui[:], 2, 511, A.logical_shift_right, A.bitwise_and, ["ui"], ["hb2"]),
            lambda: ts(T.hb[:, 0:8], T.ui[:], 3, 255, A.logical_shift_right, A.bitwise_and, ["ui"], ["hb0"]),
            lambda: ts(T.hb[:, 8:16], T.ui[:], 255, None, A.bitwise_and, None, ["ui"], ["hb1"]),
            lambda: cp(T.ho[:], T.hb[:], ["hb0", "hb1", "hb2"], ["ho", "hoF"])]
        tail_h = []
        if OPT["ffirst"] and s > 0:
            tail_h = [chain_h[4], lambda: cp(T.ho[:, 0:16], T.hb[:, 0:16], ["hb0", "hb1"], ["ho"])]
            chain_h = chain_h[0:4] + [lambda: cp(T.ho[:, 16:24], T.hb[:, 16:24], ["hb2"], ["hoF"]), lambda: None]
        chain_k = [
            lambda: cp(T.ut[:], T.M2[:, 128:136], ["M2"], ["ut"]),
            lambda: ts(T.P6[:, 56:64], T.ut[:], 2, 63, A.logical_shift_right, A.bitwise_and, ["ut"], ["P6k"]),
            lambda: ts(T.P6[:, 64:72], T.ut[:], 8, 7, A.logical_shift_right, A.bitwise_and, ["ut"], ["P6h"])]
        if s == 0:
            late = [lambda: ts(T.qb[0:8, 0:128], T.qi[0:8, :], 63, None, A.bitwise_and, None, ["qi"], ["qb0"]),
                    lambda: ts(T.qb[0:8, 128:256], T.qi[0:8, :], 6, None, A.logical_shift_right, None, ["qi"], ["qb1"]),
                    lambda: cp(T.qh[0:8, :], T.qb[0:8, :], ["qb0", "qb1"], ["qh"]),
                    lambda: ts(T.LP[:], T.awi[:], 3232.0, -6619136.0, A.mult, A.add, ["awi"], ["LP"]),
                    lambda: ts(T.Sp[:], T.swi[:], -2048.0, None, A.add, None, ["swi"], ["Sp"])]
        for ch in (OPT["hash0"] if s == 0 else OPT["hash"]):
            if ch == "h":
                chain_h.pop(0)()
            elif ch == "k":
                chain_k.pop(0)()
            else:
                fill()
        if a1:
            act(T.A1[:], T.awf[:].indirect(T.ho[:, 0:8]), AF.Identity, ["awf", "ho"], ["A1"], bias=32.0)
            if a1 == 1:
                repeat("a", 0, cut, [4])
        mm(T.M2[:, 0:128], T.idb[:], T.nbig[:, 0:128], True, False, ["idb", "nbig"], ["M2"])
        if s == 0:
            mm(T.M2[:, 0:128], T.E0[0:8, :], T.qh[0:8, 0:128], False, False, ["E0", "qh"], ["M2"])
            mm(T.M2[:, 0:128], T.E64[0:8, :], T.qh[0:8, 128:256], False, True, ["E64", "qh"], ["M2"])
        else:
            mm(T.M2[:, 0:128], T.Ex[0:16, :], Z[0:16, 1:256:2], False, True, ["Ex", zk], ["M2"])
        nF = 4 - OPT["shift"][s]
        for c in range(nF):
            mm(DD[:, 512 * c:512 * c + 512], T.NI[:, 0:128], T.zx[:, 512 * c:512 * c + 512], True, False,
               ["NI0"] + (zx_keys[0:5] if 32 * c + 32 <= cut else zx_keys[0:10]) + zall, ["D%d" % c])
        Fw, fk = (T.fwi[:], "fwi") if s == 0 else (T.FW[:, 0:512], "FW")
        chain_f = [
            lambda: tt(T.t1[:], Fw.indirect(T.ho[:, 16:24]), T.nown[:], A.mult, [fk, "hoF", "nown"], ["t1"]),
            lambda: tt(T.nf[:, 0:128], T.t1[:], T.M2[:, 0:128], A.max, ["t1", "M2"], ["nf0"]),
            lambda: cp(T.off[:, 0:128], T.nf[:, 0:128], ["nf0"], ["off0"])]
        chain_c = [
            lambda: ts(T.A1[:], T.awi[:].indirect(T.ho[:, 0:8]), 32.0, None, A.add, None, ["awi", "ho"], ["A1"]),
            lambda: tt(T.pr[:], T.Sp[:].indirect(T.ho[:, 8:16]), T.A1[:], A.mult, ["Sp", "ho", "A1"], ["pr"]),
            lambda: tt(T.xi[:], T.LP[:].indirect(T.ho[:, 0:8]), T.pr[:], A.add, ["LP", "ho", "pr"], ["xi"]),
            lambda: ts(T.ci[:], T.xi[:], 5, 4095, A.arith_shift_right, A.bitwise_and, ["xi"], ["ci"]),
            lambda: cp(T.off[:, 128:256], T.ci[:], ["ci"], ["off1"])]
        if a1:
            chain_c[0] = lambda: None
        if s == 0:
            late = [lambda: ts(T.thr[0:1, 0:8], T.thi[0:1, 0:8], 4096.0, None, A.mult, None, ["thi"], ["THa"]),
                    lambda: ts(T.thr[0:1, 8:16], T.thi[0:1, 0:8], 4096.0, None, A.mult, None, ["thi"], ["THb"])]
        for ch in (OPT["order0"] if s == 0 else OPT["order"]):
            if ch == "f":
                chain_f.pop(0)()
            elif ch == "c":
                chain_c.pop(0)()
            elif ch == "h":
                tail_h.pop(0)()
            elif ch == "k":
                chain_k.pop(0)()
            else:
                fill()
        fill(len(late))
        cp(T.nf[:, 128:256], T.ci[:], ["ci"], ["nf1"])
        if s == 0:
            race_consts()

        def old_column():
            act(T.Fr[:], T.FW[:, 0:512].indirect(T.ho[:, 16 + 4 * lam:20 + 4 * lam]), AF.Identity, ["FW", "hoF"], ["Fr"])

        def upper(r):
            act(T.hib[:, 128 * r:128 * r + 128], T.nf[:, 128 * r:128 * r + 128], AF.Identity, ["nf%d" % r], ["hib%d" % r], bias=12256.5)

        if not OPT["ffirst"] or s == 0:
            upper(0)
        VK = T.M1[:, 128:144]
        mm(VK, T.on[0:1, :], T.c1088[0:1, :], True, False, ["on", "c1088"], ["M1"])
        mm(VK, T.onef[0:1, :], T.thr[0:1, :], False, False, ["onef", "THa", "THb"], ["M1"])
        if s == 0:
            mm(VK, T.qh[0:8, 0:128], T.idb[0:8, 0:16], False, False, ["idb", "qh"], ["M1"])
            mm(VK, T.qh[0:8, 128:256], T.I8[0:8, :], False, True, ["I8", "qh"], ["M1"])
        else:
            mm(VK, T.c32[:], T.IV[:, 8:24], False, False, ["c32", "IV"], ["M1"])
            mm(VK, Z[0:16, 1:256:2], T.idb[0:16, 0:16], False, True, ["idb", zk], ["M1"])

        Xw = T.X[:, 0:4096]
        P = slice(0, 64) if last else slice(0, 128)

        def half_open(h, r):
            K, k = (T.KC, "KC") if r else (T.KF, "KF")
            o = K[64 * h:64 * h + 64, 256 * h:256 * h + 256]
            t0 = 128 * r + 64 * h
            mm(o, T.on[0:1, 0:64], T.CK[0:1, 256 * r:256 * r + 256], True, False, ["on", "CK%d" % r], [k])
            mm(o, T.hib[:, t0:t0 + 64], T.NI[:], False, False, ["hib%d" % r, "NI0", "NI1"], [k])
            mm(K[64 * h:64 * h + 64, 256 * h:256 * h + 128], T.nf[:, t0:t0 + 64], T.idf[:], False, False, ["nf%d" % r, "idf"], [k])

        def half_keys(h, K, k, src, c0, b0, rd, stop, cls=range(16)):
            for i in cls:
                mm(K[64 * h:64 * h + 64, 256 * h + i:256 * h + 256:16], src[:, c0 + 1024 * h + i:c0 + 1024 * h + 1024:16], T.Bk[:, b0:b0 + 16],
                   False, stop and i == 15, rd, [k])

        def half_f(h):
            for c in (2 * h, 2 * h + 1):
                act(T.WF[:, 512 * c:512 * c + 512], Xw.indirect(T.off[:, 32 * c:32 * c + 32]), AF.Identity, ["X", "off0"], ["WF%d" % c])
                mm(DD[:, 512 * c:512 * c + 512], T.idb[:], T.WF[:, 512 * c:512 * c + 512], False, True, ["idb", "WF%d" % c], ["D%d" % c])

        def half_abs(h, c):
            act(T.Dw[:, 1024 * h + c:1024 * h + 1024:2], DD[:, 1024 * h + c:1024 * h + 1024:2], AF.Abs, ["D%d" % (2 * h), "D%d" % (2 * h + 1)],
                ["Dw0%d" % (2 * h + c)])

        def half_c(h):
            tt(T.Dw[:, 2048 + 1024 * h:3072 + 1024 * h], Xw.indirect(T.off[:, 128 + 64 * h:192 + 64 * h]), T.zx[:, 1024 * h:1024 * h + 1024],
               A.subtract, ["X", "off1"] + zx_keys, ["Dw1" if h else "Dw10"])

        def half_relu(h):
            ts(T.RC[:, 1024 * h:1024 * h + 1024], T.Dw[:, 2048 + 1024 * h:3072 + 1024 * h], 0.0, None, A.max, None,
               ["Dw1" if h else "Dw10"], ["RC" if h else "RCa"])

        def half_race(h, now=True):
            p = slice(64 * h, 64 * h + 64)
            S1, K1, k1, S2, K2, k2 = (T.SC, T.KC, "C", T.SF, T.KF, "F") if h else (T.SF, T.KF, "F", T.SC, T.KC, "C")
            calls = [
                lambda: scan(S1[p, :], T.rmin[p, :], K1[p, 256 * h:256 * h + 256], A.add, A.min, ["rmin0", "rmin1", "K" + k1], ["S" + k1]),
                lambda: tt(T.m1[p, :], S1[p, 15:256:16], T.M1[p, 128:144], A.min, ["S" + k1, "M1"], ["m1"]),
                lambda: scan(S2[p, :], T.rmin[p, :], K2[p, 256 * h:256 * h + 256], A.add, A.min, ["rmin0", "rmin1", "K" + k2], ["S" + k2]),
                lambda: tt(T.R[p, 0:16], S2[p, 15:256:16], T.m1[p, :], A.min, ["S" + k2, "m1"], ["Rw"])]
            if now:
                for j in (0, 2, 1, 3):
                    calls[j]()
            return calls

        if last:
            half_f(0)
            act(T.hib[:], T.nf[:], AF.Identity, ["nf0", "nf1"], ["hib0", "hib1"], bias=12256.5)
            half_c(0)
            half_open(0, 0)
            half_open(0, 1)
            half_relu(0)
            half_abs(0, 0)
            half_abs(0, 1)
            half_keys(0, T.KF, "KF", T.Dw, 0, 0, ["Dw00", "Bk"], False, range(0, 16, 2))
            half_keys(0, T.KC, "KC", T.Dw, 2048, 32, ["Dw10", "Bkn"], False)
            half_keys(0, T.KF, "KF", T.Dw, 0, 0, ["Dw01", "Bk"], True, range(1, 16, 2))
            half_c(1)
            half_keys(0, T.KC, "KC", T.RC, 0, 16, ["RCa", "Bk2"], True)
            half_f(1)
            act(T.Dw[:, 1024:1536], DD[:, 1024:1536], AF.Abs, ["D2"], ["Dw02"])
            act(T.Dw[:, 1536:2048], DD[:, 1536:2048], AF.Abs, ["D3"], ["Dw03"])
            act(T.RC[:, 1024:1024 + OPT["r1"]], T.Dw[:, 3072:3072 + OPT["r1"]], AF.Relu, ["Dw1"], ["RC"])
            half_race(0)
            nF = 0
        for r, K, k in ((1, T.KC, "KC"), (0, T.KF, "KF")):
            if not last:
                mm(K[:, 0:256], T.on[0:1, :], T.CK[0:1, 256 * r:256 * r + 256], True, False, ["on", "CK%d" % r], [k])

        def names(r, K, k):
            mm(K[:, 0:256], T.hib[:, 128 * r:128 * r + 128], T.NI[:], False, False, ["hib%d" % r, "NI0", "NI1"], [k])
            mm(K[:, 0:128], T.nf[:, 128 * r:128 * r + 128], T.idf[:], False, False, ["nf%d" % r, "idf"], [k])

        for c in range(nF):
            act(T.WF[:, 512 * c:512 * c + 512], Xw.indirect(T.off[:, 32 * c:32 * c + 32]), AF.Identity, ["X", "off0"], ["WF%d" % c])
            mm(DD[:, 512 * c:512 * c + 512], T.idb[:], T.WF[:, 512 * c:512 * c + 512], False, True, ["idb", "WF%d" % c], ["D%d" % c])
            if OPT["ffirst"] and s > 0:
                if c == nF - 1:
                    act(T.hib[:], T.nf[:], AF.Identity, ["nf0", "nf1"], ["hib0", "hib1"], bias=12256.5)
                    names(1, T.KC, "KC")
                    names(0, T.KF, "KF")
                continue
            if c == 0:
                names(0, T.KF, "KF")
            if c == min(1, nF - 1):
                upper(1)
            if c == nF - 1:
                names(1, T.KC, "KC")
        light = OPT["light"]
        if last:
            dw0 = ["Dw0%d" % c for c in range(4)] + ["Dw0s"]
        elif light:
            for h in range(2):
                tt(T.Dw[:, 2048 + 1024 * h:3072 + 1024 * h], Xw.indirect(T.off[:, 128 + 64 * h:192 + 64 * h]), T.zx[:, 1024 * h:1024 * h + 1024],
                   A.subtract, ["X", "off1"] + zx_keys, ["Dw1%d" % h] + (["Dw1"] if h else []))
            for c in range(nF, 4):
                tt(T.WF[:, 512 * c:512 * c + 512], Xw.indirect(T.off[:, 32 * c:32 * c + 32]), T.zx[:, 512 * c:512 * c + 512], A.subtract,
                   ["X", "off0"] + zx_keys, ["WF%d" % c])
            if s == 0:
                old_column()
            act(T.Dw[:, 0:512 * nF], DD[:, 0:512 * nF], AF.Abs, ["D%d" % j for j in range(nF)], ["Dw0s"])
            for h in range(2):
                act(T.RC[:, 1024 * h:1024 * h + 1024], T.Dw[:, 2048 + 1024 * h:3072 + 1024 * h], AF.Abs, ["Dw1%d" % h], ["RC%d" % h])
            for c in range(nF, 4):
                act(T.Dw[:, 512 * c:512 * c + 512], T.WF[:, 512 * c:512 * c + 512], AF.Abs, ["WF%d" % c], ["Dw0%d" % c])
            dw0 = ["Dw0s", "Dw10", "Dw11"] + ["Dw0%d" % c for c in range(4)]
            for i in range(16):
                mm(T.KC[:, i:256:16], T.RC[:, i:2048:16], T.Bk[:, 0:16], False, i == 15, ["RC0", "RC1", "Bk"], ["KC"])
            for i in range(16):
                mm(T.KF[:, i:256:16], T.Dw[:, i:2048:16], T.Bk[:, 0:16], False, i == 15, dw0 + ["Bk"], ["KF"])
        else:
            if nF < 4:
                tt(T.WF[:, 512 * nF:2048], Xw.indirect(T.off[:, 32 * nF:128]), T.zx[:, 512 * nF:2048], A.subtract,
                   ["X", "off0"] + zx_keys, ["WF%d" % c for c in range(nF, 4)])
                act(T.Dw[:, 512 * nF:2048], T.WF[:, 512 * nF:2048], AF.Abs, ["WF%d" % j for j in range(nF, 4)], ["Dw0s"])
            rs = OPT["rs"][s]
            if rs:
                tt(T.Dw[:, 2048:2048 + rs], Xw.indirect(T.off[:, 128:128 + rs // 16]), T.zx[:, 0:rs], A.subtract,
                   ["X", "off1"] + zx_keys, ["Dw10"])
                act(T.RC[:, 0:rs], T.Dw[:, 2048:2048 + rs], AF.Relu, ["Dw10"], ["RCa"])
            tt(T.Dw[:, 2048 + rs:4096], Xw.indirect(T.off[:, 128 + rs // 16:256]), T.zx[:, rs:2048], A.subtract,
               ["X", "off1"] + zx_keys, ["Dw1"] + ([] if rs else ["Dw10"]))
            for i in range(16):
                mm(T.KC[:, i:256:16], T.Dw[:, 2048 + i:4096:16], T.Bk[:, 32:48], False, False, ["Dw1", "Dw10", "Bkn"], ["KC"])
            ts(T.RC[:, rs:2048], T.Dw[:, 2048 + rs:4096], 0.0, None, A.max, None, ["Dw1"], ["RC"] + ([] if rs else ["RCa"]))
            nc = OPT["classes"]
            for c in range(nc):
                act(T.Dw[:, c:512 * nF:nc], DD[:, c:512 * nF:nc], AF.Abs, ["D%d" % j for j in range(nF)], ["Dw0%d" % c])
            if s > 0:
                old_column()
            dw0 = ["Dw0%d" % c for c in range(nc)] + ["Dw0s"]
            for c in range(nc):
                if c == OPT["kfirst"]:
                    for i in range(16):
                        mm(T.KC[:, i:256:16], T.RC[:, i:2048:16], T.Bk[:, 16:32], False, i == 15, ["RC", "RCa", "Bk2"], ["KC"])
                for i in range(c, 16, nc):
                    mm(T.KF[:, i:256:16], T.Dw[:, i:2048:16], T.Bk[:, 0:16], False, i == 15, ["Dw0%d" % c, "Bk", "Dw0s"], ["KF"])

        def greatest():
            scan(T.Dw[:, 4096:6144], T.rM[:], T.Dw[:, 2048:4096], A.min, A.max, ["rM", "Dw1", "Dw10", "Dw11"], ["Dw2"])

        if not last:
            greatest()
            scan(T.SC[:], T.rmin[:], T.KC[:, 0:256], A.add, A.min, ["rmin0", "rmin1", "KC"], ["SC"])
            tt(T.m1[:], T.SC[:, 15:256:16], VK, A.min, ["SC", "M1"], ["m1"])
            scan(T.SF[:], T.rmin[:], T.KF[:, 0:256], A.add, A.min, ["rmin0", "rmin1", "KF"], ["SF"])
            tt(T.R[:, 0:16], T.SF[:, 15:256:16], T.m1[:], A.min, ["SF", "m1"], ["Rw"])
        if s == 0:
            learn_consts_a()
        if s == 1:
            lin(T.id64[:], T.idb[:], 64.0, 0.0, ["idb"], ["id64"])

        pay = None if last else T["pay%d" % s]
        pk = "pay%d" % s

        def loser():
            tt(T.R[P, 16:32], T.SF[P, 15:256:16], T.SC[P, 15:256:16], A.max, ["SF", "SC"], ["Rl"])

        def place():
            ts(T.P6[:, 0:8], T.R[:, 0:8], 6, 15, A.logical_shift_right, A.bitwise_and, ["Rw"], ["V0"])

        def route():
            ts(T.P6[:, 8:24], T.R[:, 0:16], 3072, None, A.bitwise_and, None, ["Rw"], ["V1"])

        def move_b():
            mm(DD[:, 0:8], T.o16[:], T.G8[:, 0:8], True, False, ["o16", "G8a"], ["D0"])
            tt(T.E[:], T.P6[:, 0:16].indirect(T.ZO[:, 0:16]), T.own[:], A.mult, ["V0", "V1", "ZO0", "own0", "own1"], ["E"])
            mm(DD[:, 0:8], T.E[:, 0:128], T.G8[:, 0:8], False, False, ["E", "G8a"], ["D0"])
            mm(DD[:, 0:8], T.E[:, 128:256], T.G8[:, 8:16], False, True, ["E", "G8b"], ["D0"])

        def move_q():
            if last:
                mm(T.M2[0:8, 0:128], T.Pb[:, 24:32], T.idb[:], True, False, ["Pbw", "idb"], ["M2"])
                mm(T.M2[0:8, 0:128], T.Pb[:, 32:40], T.id64[:], False, True, ["Pbw", "id64"], ["M2"])
            else:
                mm(T.M2[0:16, 0:128], T.Pb[:, 24:40], T.idb[:], True, True, ["Pbw", "idb"], ["M2"])

        def move_p():
            cp(pay[0:16, 1:256:2], T.M2[0:16, 0:128], ["M2"], [pk + "q"])

        def move_o():
            cp(T.zo[:], DD[:, 0:8], ["D0"], ["zo"])

        def move_z():
            rd = dw0 + ["Dw1", "Dw10", "Dw2", "zo", "ZS"]
            if last:
                act(T.zout[:], T.Dw[:].indirect(T.zo[:]), AF.Abs, rd, ["zout"], scale=ZS)
                dma("a", T.yz[:], T.zout[:], ["zout"], [])
            else:
                act(pay[:, 0:256:2], T.Dw[:].indirect(T.zo[:]), AF.Abs, rd + ["ZB"], [pk + "z"], scale=ZS, bias=ZB)

        i2 = ["I2%da" % lam, "I2%db" % lam]
        I2 = [T.I2[P, 128 * lam:128 * lam + 64], T.I2[P, 128 * lam + 64:128 * lam + 128]]
        J, jk, j0 = (T.M2, "M2", 256) if last else (T.KC, "KC", 0)

        def flag_w():
            ts(T.IV[:, 8:24], T.P6[:, 8:24], 2048.0, 128.0, A.is_ge, A.mult, ["V1"], ["IV"])

        def flag_k():
            ts(T.IK[:, 8:16], T.P6[:, 8:16], 1024.0, 128.0, A.not_equal, A.mult, ["V1"], ["IK"])

        def keys(name, a, b):
            return [name + str(k) for k in range(a, b)]

        def compact(h, a, b):
            c0, bank = (1024, "D2") if h == 0 else (512, "D1")
            for k in range(a, b):
                o = DD[0:16, c0 + 64 * k:c0 + 64 * k + 64]
                mm(o, T.Pb[P, 24 + 16 * k:40 + 16 * k], I2[h], True, False, [("Pbw", "Pbl", "Pbk")[k], i2[h]], [bank])
                if k < 2:
                    mm(o, T.IV[P, 0:16], I2[h], False, True, ["IV", "IVz", i2[h]], [bank])
                else:
                    mm(o, T.IK[P, :], I2[h], False, True, ["IK", "IKz", i2[h]], [bank])

        def copy_asc(a, b, on_vector=False):
            o, src = T.CP[0:16, 256 + 64 * a:256 + 64 * b], DD[0:16, 512 + 64 * a:512 + 64 * b]
            if on_vector:
                cp(o, src, ["D1"], keys("CPa", a, b))
            else:
                act(o, src, AF.Identity, ["D1"], keys("CPa", a, b))

        def copy_desc(a, b):
            act(T.CP[0:16, 64 * a:64 * b], DD[0:16, 1024 + 64 * a:1024 + 64 * b], AF.Identity, ["D2"], keys("CPd", a, b))

        def spread_pe(a, b):
            mm(DD[:, 1536 + 64 * a:1536 + 64 * b], T.Ex[0:16, :], T.CP[0:16, 256 + 64 * a:256 + 64 * b], False, True, ["Ex"] + keys("CPa", a, b), ["D3"])
            mm(T.M1[:, 256 + 64 * a:256 + 64 * b], T.Ex[0:16, :], T.CP[0:16, 64 * a:64 * b], True, True, ["Ex"] + keys("CPd", a, b), ["M1"])

        def spread_v(a, b):
            scan(T.SO[:, 64 * a:64 * b], T.rneg[:, 64 * a:64 * b], DD[:, 1536 + 64 * a:1536 + 64 * b], A.add, A.max, ["rneg", "D3"], keys("SO", a, b))

        def spread_a(a, b):
            act(T.RO[:, 64 * a:64 * b], T.M1[:, 256 + 64 * a:256 + 64 * b], AF.Identity, ["M1"], keys("RO", a, b))
            lin(T.nb[:, 4 * a:4 * b], T.SO[:, 64 * a + 15:64 * b:16], -8192.0, 0.0, keys("SO", a, b), keys("nb", a, b))

        def spread_mask(a, b):
            mm(DD[:, 1536 + 64 * a:1536 + 64 * b], T.idb[:], T.nbig[:, 64 * a:64 * b], True, False, ["idb", "nbig"], ["D3"])

        def differ(seg, on_vector):
            k = seg // 4
            o, src = T.EQ[:, 64 * seg:64 * seg + 64], T.RO[:, 64 * k:64 * k + 64]
            if on_vector:
                ts(o, src, T.SO[:, 16 * seg + 15:16 * seg + 16], 8192.0, A.not_equal, A.mult, ["RO%d" % k, "SO%d" % k], ["EQ%d" % seg])
            else:
                act(o, src, AF.Abs, ["RO%d" % k, "nb%d" % k], ["EQ%d" % seg], scale=8192.0, bias=T.nb[:, seg:seg + 1])

        def first(a, b):
            scan(T.SD[:, 256 * a:256 * b], T.EQ[:, 256 * a:256 * b], T.cm[:, 256 * a:256 * b], A.min, A.max,
                 ["cm%d" % k for k in range(a, b)] + ["EQ%d" % j for j in range(4 * a, 4 * b)], ["SD%d" % k for k in range(a, b)])

        def lists(a, b):
            ks = range(a, b)
            return [lambda: lists_a(a, b, ks), lambda: lists_b(a, b, ks), lambda: lists_c(a, b, ks)]

        def lists_a(a, b, ks):
            tt(T.to[:, 4 * a:4 * b], T.SO[:, 64 * a + 15:64 * b:16], T.SD[:, 256 * a + 63:256 * b:64], A.subtract,
               keys("SO", a, b) + ["SD%d" % k for k in ks], ["to%d" % k for k in ks])

        def lists_b(a, b, ks):
            tt(T.tm[:, 4 * a:4 * b], T.to[:, 4 * a:4 * b], T.DU[:, 4 * a:4 * b], A.min, ["DU"] + ["to%d" % k for k in ks], ["tm%d" % k for k in ks])

        def lists_c(a, b, ks):
            ts(T.LO[:, 4 * a:4 * b], T.tm[:, 4 * a:4 * b], 8192.0, None, A.add, None, ["tm%d" % k for k in ks], ["LO%d" % k for k in ks])

        def slow_a():
            scan(T.SX[P, :], T.rmax[P, :], T.KF[P, 0:128], A.add, A.max, ["rmax", "KF"], ["SX"])

        def slow_b():
            cp(T.jt[:], T.SX[:, 15:128:16], ["SX"], ["jt"])

        def slow_c():
            ts(T.P6[:, 72:80], T.jt[:], 6, 63, A.logical_shift_right, A.bitwise_and, ["jt"], ["P6j"])

        def slow_d():
            cp(T.Pb[:, 72:80], T.P6[:, 72:80], ["P6j"], ["Pbj"])

        def slow_e():
            mm(J[0:16, j0:j0 + 64], T.Pb[P, 72:88], I2[1], True, True, ["Pbj", "Pbz", i2[1]], [jk])

        def slow_f():
            act(T.CP[0:16, 192:256], J[0:16, j0:j0 + 64], AF.Identity, [jk], ["CPj"])

        def slow_g():
            mm(J[:, j0 + 64:j0 + 192], T.Ex[0:16, :], T.CP[0:16, 192:320], True, True, ["Ex", "CPj", "CPa0"], [jk])

        def col_a():
            tt(T.d1[:], J[:, j0 + 128:j0 + 192], T.Fr[:], A.subtract, [jk, "Fr"], ["d1"])

        def col_b():
            ts(T.oh[:], J[:, j0 + 64:j0 + 128], JC, None, A.is_equal, None, [jk, "JC"], ["oh"])

        def col_c():
            tt(T.d2[:], T.d1[:], T.oh[:], A.mult, ["d1", "oh"], ["d2"])

        def col_d():
            tt(T.FW[:].indirect(T.LO[:, 8:12]), T.Fr[:], T.d2[:], A.add, ["Fr", "d2", "LO2"], ["FW", "FWd"])

        new_words = [
            lambda: tt(T.te[:], T.SO[:, 15:128:16], T.DU[:, 16:24], A.min, ["SO0", "SO1", "DUe"], ["te"]),
            lambda: cp(T.LE[:], T.te[:], ["te"], ["LE"]),
            lambda: tt(T.xs[:], T.X[:].indirect(T.LE[:, 0:4]), zc(64 * lam, 64 * lam + 64), A.add, ["X", "Xd", "LE", zk], ["xs"]),
            lambda: ts(T.xl[:], T.X[:].indirect(T.LE[:, 4:8]), CD, 0.0, A.add, A.max, ["X", "Xd", "LE", "CD"], ["xl"]),
            lambda: ts(T.xh[:], T.xs[:], C1, C2 if s == 0 else C3, A.mult, A.add, ["xs", "C1", "C2", "C3"], ["xh"]),
            lambda: ts(T.xw[:], T.xh[:], CMX, None, A.min, None, ["xh", "CMX"], ["xw"])]

        def put_l():
            cp(T.X[:].indirect(T.LO[:, 4:8]), T.xl[:], ["xl", "LO1"], ["X", "Xd"])

        def put_w():
            cp(T.X[:].indirect(T.LO[:, 0:4]), T.xw[:], ["xw", "LO0"], ["X", "Xd"])

        def dedupe(plan, segs):
            nv = plan.count("e")
            todo = list(segs[:nv])
            for seg in segs[nv:]:
                differ(seg, False)
            for ch in plan:
                if ch == "w":
                    new_words.pop(0)()
                elif ch == "e":
                    differ(todo.pop(0), True)
                elif ch == "a":
                    col_a()
                elif ch == "b":
                    col_b()
                elif ch == "c":
                    col_c()

        if not last:
            place()
            route()
            ts(T.P6[:, 24:40], T.R[:, 0:16], 63, None, A.bitwise_and, None, ["Rw"], ["P6w"])
            move_b()
            cp(T.Pb[:, 8:40], T.P6[:, 8:40], ["P6w", "V1"], ["Pbw"])
            move_q()
            loser()
            move_o()
            move_p()
            move_z()
            order("g", [pk + "z", pk + "q"], [])
            tr = []
            sent = 0
            for b, (dst, m, per) in enumerate(travel_engines(T, topo, rank, s)):
                rid, pid = topo.addr(dst)[0], topo.addr(dst)[1]
                tr.append(RemoteDMATransfer(dst_ids=[DstId(rid=rid, pnc=pid)], dma_engine_mask=m, remote_sem=T.sem["arr%d" % (s + 1)],
                                            src=pay[:, 64 * b:64 * b + 64], dst=T["L%d" % (s + 1)][:, 64 * b:64 * b + 64]))
                sent += per
            g.remote_dma_fused(tr, local_sem=T.sem["sent%d" % s])
            count["sent%d" % s] = sent
            ts(T.P6[:, 40:56], T.R[:, 16:32], 63, None, A.bitwise_and, None, ["Rl"], ["P6l"])
            flag_w()
            flag_k()
            cp(T.Pb[:, 40:72], T.P6[:, 40:72], ["P6l", "P6k", "P6h"], ["Pbl", "Pbk"])
            if s == 0:
                later_consts()
                tt(T.Ex[0:16, :], T.E0[0:16, :], T.E8[0:16, :], A.add, ["E0", "E8"], ["Ex"])
                learn_consts_b()
            spread_mask(0, 3)
            compact(1, 0, 3)
            compact(0, 0, 3)
            slow_a()
            copy_asc(0, 3, True)
            copy_desc(0, 3)
            slow_b()
            spread_pe(0, 3)
            slow_c()
            spread_v(0, 3)
            slow_d()
            spread_a(0, 3)
            if s == 0:
                cp(T.FW[:, 0:512], T.fwi[:], ["fwi"], ["FW"])
                old_column()
            slow_e()
            slow_f()
            slow_g()
            dedupe(OPT["plan"], list(range(12)))
            ls = lists(0, 3)
            tail = [lambda: first(0, 3), col_a, ls[0], col_b, ls[1], col_c, ls[2], col_d, put_l, put_w]
            while len(tail) > OPT["defer"]:
                tail.pop(0)()
            return tail
        loser()
        route()
        ts(T.P6[:, 24:56], T.R[:], 63, None, A.bitwise_and, None, ["Rw", "Rl"], ["P6w", "P6l"])
        flag_w()
        cp(T.Pb[:, 24:72], T.P6[:, 24:72], ["P6w", "P6l", "P6k", "P6h"], ["Pbw", "Pbl", "Pbk"])
        spread_mask(0, 2)
        compact(1, 0, 2)
        compact(0, 0, 2)
        flag_k()
        slow_a()
        if OPT["r1"] < 1024:
            ts(T.RC[:, 1024 + OPT["r1"]:2048], T.Dw[:, 3072 + OPT["r1"]:4096], 0.0, None, A.max, None, ["Dw1"], ["RCb"])
        copy_asc(0, 2, True)
        copy_desc(0, 2)
        slow_b()
        spread_pe(0, 2)
        spread_v(0, 2)
        spread_a(0, 2)
        slow_c()
        compact(1, 2, 3)
        compact(0, 2, 3)
        half_open(1, 1)
        half_keys(1, T.KC, "KC", T.Dw, 2048, 32, ["Dw1", "Bkn"], False)
        dedupe(OPT["last_plan"], list(range(8)))
        copy_asc(2, 3)
        copy_desc(2, 3)
        spread_mask(2, 3)
        spread_pe(2, 3)
        first(0, 2)
        lx, lf = lists(0, 2), lists(2, 3)
        half_keys(1, T.KC, "KC", T.RC, 0, 16, ["RC", "RCb", "Bk2"], True)
        old_column()
        for call in (slow_d, lx[0], lambda: spread_v(2, 3), lx[1], slow_e, slow_f, slow_g, lx[2], lambda: spread_a(2, 3), put_l, put_w):
            call()
        half_open(1, 0)
        half_keys(1, T.KF, "KF", T.Dw, 0, 0, ["Dw02", "Dw03", "Bk"], True)
        dma("s", T.yx[:], T.X[:, 0:4096], ["X"], [])
        for seg in range(8, 12):
            differ(seg, False)
        hr = half_race(1, False)
        for call in (hr[0], lambda: first(2, 3), hr[1], col_a, hr[2], lf[0], hr[3], col_b, lf[1], place, route, col_c, lf[2], move_b, col_d):
            call()
        dma("s", T.yf[:], T.FW[:, 0:512], ["FW"], [])
        ts(T.P6[:, 24:40], T.R[:, 0:16], 63, None, A.bitwise_and, None, ["Rw"], ["P6w"])
        greatest()
        cp(T.Pb[:, 24:40], T.P6[:, 24:40], ["P6w"], ["Pbw"])
        move_q()
        move_o()
        move_z()
        act(T.qout[0:8, :], T.M2[0:8, 0:128], AF.Identity, ["M2"], ["qout"])
        dma("s", T.yq[:], T.qout[0:8, :], ["qout"], [])
        return []

    rest = []
    for s in range(STEPS):
        rest = step(s, rest)

    for sem, val in count.items():
        g.wait_ge(T.sem[sem], val)
